import numpy as np, ml_dtypes
CORES = [2,6,10,14,18,22,26,30]
N = 8
import mx_ref
BF = ml_dtypes.bfloat16
def pick(q, e):
    c = np.concatenate([q[0].reshape(128, -1, 4), np.zeros((128, 1, 4), np.uint8)], axis=1); s = np.concatenate([q[1], np.ones((16, 1), np.uint8)], axis=1)
    return (np.ascontiguousarray(c[:, e].reshape(128, -1)), np.ascontiguousarray(s[:, e]))
def join(*qs):
    return (np.concatenate([q[0] for q in qs], axis=1), np.concatenate([q[1] for q in qs], axis=1))
def put(q, e, v):
    c, s = q[0].reshape(128, -1, 4).copy(), q[1].copy(); c[:, e] = v[0].reshape(128, -1, 4); s[:, e] = v[1]
    return (c.reshape(128, -1), s)
def pk(c, s):
    return (np.ascontiguousarray(c), mx_ref.live(s))
def emit(q):
    return q[0], q[1]
def cols(t, e):
    v = np.concatenate([t.reshape(128, -1, 4), np.zeros((128, 1, 4), BF)], axis=1)
    return np.ascontiguousarray(v[:, e]).reshape(128, -1)
def tile(rs):
    return np.stack(rs, axis=2).reshape(128, -1).astype(BF)
def cut(t, i, w=512):
    return t[:, w * i:w * i + w]
def f(rng, *shape):
    return mx_ref.flush((rng.standard_normal(shape, dtype=np.float32) * np.exp2(rng.integers(-2, 3, shape[:-1] + (1,)))).astype(BF))
def wide(rng, *shape, cols=0):
    v = rng.standard_normal(shape, dtype=np.float32) * np.exp2(rng.integers(-12, 13, shape)).astype(np.float32)
    if cols: v *= np.repeat(np.exp2(rng.integers(-cols, cols + 1, shape[:-2] + (1, shape[-1] // 4))) * (rng.random(shape[:-2] + (1, shape[-1] // 4)) > 0.0625), 4, axis=-1).astype(np.float32)
    return mx_ref.flush(v.astype(BF))
T, CAPP, CB, DF = 128, 32, 16, 64
LEVELS = np.array([0, 16, 32, 64], np.float32)
def taken(first, a):
    return np.concatenate([s * T + np.flatnonzero(first[s] == a)[:CAPP] for s in range(N)])
def plain(rng):
    rt, r2 = np.array(f(rng, 128, 512)), np.zeros((128, 512), BF)
    rt[:, 4 * N:] = 0
    v = f(rng, 128, 4 * N + 4).astype(np.float32).reshape(128, N + 1, 4)
    v = v - np.mean(v, axis=(0, 2), keepdims=True)
    r2[:, :4 * N + 4] = mx_ref.flush(v.reshape(128, -1).astype(BF))
    return {"x": np.array(f(rng, N, 128, 4 * T)), "rt": np.stack([rt] * N), "w": np.array(f(rng, N, 128, 2048)), "r2": np.stack([r2] * N), "vx": f(rng, N, 128, 512), "vh": f(rng, N, 128, 512)}
def planned(rng, A, B, V, dead=None, same=False):
    d = plain(rng)
    rt, r2, wt = d["rt"], d["r2"], d["w"].reshape(N, 128, 4, 128, 4)
    rt[:, 120:] = 0
    r2[:, :4 * N + 4] = 0
    wt[:, 120:] = 0
    for k in range(N + 1):
        r2[:, 4 * k:4 * k + 4, 4 * k:4 * k + 4] = 32
        wt[:, 120 + k // 4, :, 4 * k:4 * k + 4, k % 4] = 64
    k = N + 1
    wt[:, 120 + k // 4, :, :, k % 4] = -64
    if same:
        p = f(rng, 128, 4 * N)
        x = np.stack([cols(p, A[s]) for s in range(N)])
    else: x = f(rng, N, 128, 4 * T)
    x = np.array(x, np.float32).reshape(N, 128, T, 4)
    g = rt[0].astype(np.float32).reshape(128, 128, 4)
    for s in range(N): x[s] = x[s] + g[:, A[s]]
    x[:, 120:] = 0
    s, j = np.nonzero(B >= 0)
    b = B[s, j]
    x[s, 120 + b // 4, j, b % 4] = 64
    x[:, 120 + N // 4, :, N % 4] = LEVELS[V]
    if dead is not None: x[:, 120 + k // 4, :, k % 4] = np.where(dead, 256, 0)
    d["x"] = np.array(mx_ref.flush(x.reshape(N, 128, 4 * T).astype(BF)))
    return d
def choose(rng, A):
    B, V = (A + 1 + rng.integers(0, N - 1, A.shape)) % N, np.zeros((N, T), int)
    for a in range(N):
        k = taken(A, a)
        V.flat[k] = 3
        k = rng.permutation(k)[:DF]
        V.flat[k] = 0
        B.flat[k] = np.resize(rng.permutation([b for b in range(N) if b != a]), len(k))
    return B, V
def setup_inputs(rng):
    return plain(rng)
def setup_inputs_crowd(rng):
    h, A = int(rng.integers(1, N - 1)), []
    o = (int(rng.choice([i for i in range(1, N) if i not in (h, h + 1)])), h)
    for s in range(N):
        one, two, e = (s + o[0]) % N, (s + o[1]) % N, int(rng.integers(1, 9))
        rest = [a for a in range(N) if a not in (one, two, (two + 1) % N)]
        A.append(rng.permutation(np.concatenate([np.full(CAPP, one), np.full(CAPP + e, two), np.resize(rng.permutation(rest), T - 2 * CAPP - e)])))
    A = np.stack(A)
    B, V = choose(rng, A)
    for a in range(N):
        one, two, e = (a + o[0]) % N, (a + o[1]) % N, int(rng.integers(1, CB // 4 + 1))
        rest = [b for b in range(N) if b not in (a, one, two)]
        k = taken(A, a)
        k = rng.permutation(k[V.reshape(-1)[k] == 0])
        B.flat[k] = np.concatenate([np.full(CB, one), np.full(CB + e, two), np.resize(rng.permutation(rest), len(k) - 2 * CB - e)])
    return planned(rng, A, B, V)
def setup_inputs_few(rng):
    none, less, even, full = rng.permutation(N)[:4]
    act, n = [a for a in range(N) if a not in (none, less, even, full)] or [full], DF // (2 * N)
    fix = np.concatenate([np.full(n, less), np.full(2 * n, even), np.full(CAPP + 4, full)])
    A = np.stack([rng.permutation(np.concatenate([fix, np.resize(rng.permutation(act), T - len(fix))])) for s in range(N)])
    B, V = choose(rng, A)
    m = (A == less) | (A == even)
    V[m] = rng.integers(0, 4, int(np.count_nonzero(m)))
    k = taken(A, full)
    V.flat[k] = 3
    k = np.concatenate([k[-16::5], rng.permutation(k[:-16])[:DF - 4]])
    V.flat[k] = 0
    B.flat[k] = np.resize(rng.permutation([b for b in range(N) if b != full]), DF)
    d = planned(rng, A, B, V)
    p, t = 120 + (N + 2) // 4, (N + 2) % 4
    d["x"][:, p, t::4] = 64
    d["w"].reshape(N, 128, 4, 128, 4)[:, p, :, 4 * N + 4:4 * N + 8, t] = 64
    d["r2"][:, 4 * N + 4:4 * N + 8] = 0
    d["r2"][:, 4 * N + 4:4 * N + 8, :4 * N] = -64
    d["x"] = (d["x"].astype(np.float32) * np.float32(2.0 ** 21)).astype(BF)
    d["r2"] = (d["r2"].astype(np.float32) * np.float32(2.0 ** 24)).astype(BF)
    return d
def setup_inputs_ties(rng):
    lo, hi = np.sort(rng.permutation(N)[:2])
    k = int(rng.choice([i for i in range(N - 1) if i != hi]))
    act = [a for a in range(N) if a != hi]
    A = np.stack([rng.permutation(np.resize(rng.permutation(act), T)) for s in range(N)])
    B, V, c = np.zeros((N, T), int), np.full((N, T), 3), 3 * (DF // 6)
    for a in act:
        g = rng.permutation(taken(A, a))
        n = (len(g) - 2 * c) // 3
        B.flat[g] = (a + 1) % N
        V.flat[g[:c]] = 0
        B.flat[g[c:2 * c]] = (a + 2) % N
        V.flat[g[c:2 * c]] = 1
        B.flat[g[2 * c:2 * c + 3 * n]] = (a + 3 + np.repeat(np.arange(n), 3) % (N - 3)) % N
        V.flat[g[2 * c:2 * c + 3 * n]] = 2
    d = planned(rng, A, B, V, same=True)
    d["rt"][:, :, 4 * hi:4 * hi + 4] = d["rt"][:, :, 4 * lo:4 * lo + 4]
    d["r2"][:, 4 * k + 4:4 * k + 8, 4 * k:4 * k + 4] = 32
    d["r2"][:, :, 4 * k + 4:4 * k + 8] = d["r2"][:, :, 4 * k:4 * k + 4]
    return d
def setup_inputs_zero(rng):
    A = np.stack([rng.permutation(np.resize(np.arange(N), T)) for s in range(N)])
    B, V, dead = (A + 1 + rng.integers(0, N - 1, A.shape)) % N, np.full((N, T), 3), np.zeros((N, T), bool)
    for a in range(N):
        k = rng.permutation(taken(A, a))
        z = DF // 2 if a % 2 else DF + DF // 8
        dead.flat[k[:z]] = True
        B.flat[k[:z]] = -1
        V.flat[k[:z]] = 0
        g = k[z:DF]
        if len(g):
            V.flat[g] = 1
            B.flat[g] = np.resize(rng.permutation([b for b in range(N) if b != a]), len(g))
        if a == 0: blank = k[:z:2]
    d = planned(rng, A, B, V, dead=dead)
    nil = np.where(d["rt"][0, :, :4].astype(np.float32) < 0, np.float32(0.0), np.float32(-0.0)).astype(BF)
    for i in blank: d["x"][i // T, :, 4 * (i % T):4 * (i % T) + 4] = nil
    return d
def setup_inputs_spread(rng):
    return {**plain(rng), "x": wide(rng, N, 128, 4 * T, cols=4)}
def check_inputs(d):
    b = []
    for k in ("x", "rt", "w", "r2", "vx", "vh"):
        v = np.abs(d[k].astype(np.float32))
        if not (np.isfinite(v).all() and ((v == 0) | (v >= 2.0 ** -30) & (v <= 2.0 ** 30)).all()): b.append("a value of " + k)
    for k, n in (("rt", N), ("r2", N + 1)):
        v = d[k].astype(np.float32)
        if (v[:, :, 4 * n:] != 0).any(): b.append(k + " has numbers behind its first columns")
        if (v != v[:1]).any(): b.append(k + " differs between ranks")
    return b
def reference(x, rt, w, r2, vx, vh):
    q = [mx_ref.quantize(np.ascontiguousarray(x[s])) for s in range(N)]
    every = join(*q)
    first = np.stack([np.argmax(mx_ref.matmul(mx_ref.quantize(np.ascontiguousarray(rt[s])), q[s])[:N] + np.float32(0.0), axis=0) for s in range(N)])
    who, at, made = np.full((N, N * CB), -1), np.full((N, N * CB), -1), []
    for a in range(N):
        k = taken(first, a)
        t = pick(every, np.concatenate([k, np.full(N * CAPP - len(k), -1)]))
        z = [mx_ref.matmul(mx_ref.quantize(np.ascontiguousarray(cut(w[a], i))), t) for i in range(4)]
        h = mx_ref.quantize(np.ascontiguousarray(tile([np.maximum(v, np.float32(0.0)) * np.float32(0.0625) for v in z])))
        made.append(h)
        e = mx_ref.matmul(mx_ref.quantize(np.ascontiguousarray(r2[a])), h)[:N + 1, :len(k)] + np.float32(0.0)
        late = np.sort(np.argsort(e[N], kind="stable")[:DF])
        e[a] = -np.inf
        second = np.argmax(e[:N], axis=0)
        for b in range(N):
            m = late[second[late] == b][:CB]
            who[b, a * CB:a * CB + len(m)] = k[m]
            at[b, a * CB:a * CB + len(m)] = a * N * CAPP + m
    made = join(*made)
    y, oc, osc = np.zeros((N, 128, N * CB), np.float32), np.zeros((N, 128, 4 * N * CB), np.uint8), np.zeros((N, 16, N * CB), np.uint8)
    for b in range(N):
        t, h = pick(every, who[b]), pick(made, at[b])
        v = mx_ref.matmul(mx_ref.quantize(np.ascontiguousarray(vx[b])), t) + mx_ref.matmul(mx_ref.quantize(np.ascontiguousarray(vh[b])), h)
        y[b] = np.where(who[b] >= 0, v, np.float32(0.0))
        oc[b], osc[b] = emit(h)
    return {"y": y, "who": who.astype(np.float32).reshape(N, 1, N * CB), "oc": oc, "osc": osc}

@@ -1,0 +1,363 @@
+from concourse.bass import DstId, RemoteDMATransfer
+from concourse.mybir import dt, AluOpType as A, AxisListType, ActivationFunctionType as F
+
+N = 8
+TK = 128
+CAPP = 32
+CB = 16
+DF = 64
+SL = N * CAPP
+HO = 384
+XW = 642
+BIG = 1e29
+OUT = 100.0
+
+SCRATCH = {}
+
+
+def _declare(kind, dtype, **bufs):
+    for name, n in bufs.items():
+        SCRATCH[name] = (kind, n if isinstance(n, list) else [128, n], dtype)
+
+
+_declare("sbuf", "bfloat16", xt=520, rtt=512, wt=2048, r2t=512, r8t=512, vxt=512, vht=512, zt=512, ht=1032)
+_declare("sbuf", "float8_e4m3fn_x4", xq=136, rq=128, wq=512, r2q=128, r8q=128, vxq=128, vhq=128, sq=SL, xh=648, s2q=SL, l2q=SL, hq=128)
+_declare("sbuf", "uint8", xs=136, rs=128, ws=512, r2s=128, r8s=128, vxs=128, vhs=128, ss=SL, xhs=648, s2s=SL, l2s=SL, hs=128)
+_declare("dram", "bfloat16", fd=[128, 1], fl=[N, 128, 1], tokd=[N, 128, 1], tokl=[N, 128, 1])
+_declare("dram", "float32", whod=[N, 128, 1], whol=[N, 128, 1])
+_declare("sbuf", "int32", pp=8, cc=8, ia=8, ib=8, ic=8, ie=8, ig=8, p15=8, p31=8, px=8, pb=8)
+_declare("sbuf", "float32", thr1=2, thr2=2, xadd=1, ccol=1, ecol=2, mcol=2, mgt=2, neg8=8, zf=128, tri=128, io32=32, base=SL, m1=128)
+_declare("sbuf", "bfloat16", zb=128, rsA=512, rsB=1024, rsC=768, tokv=144)
+_declare("sbuf", "uint16", offz=2, offh=8, off1=16, off2=16)
+_declare("sbuf", "float32", R=8, lt=8, first=1, of1=16, of2=16, tokw=648, nb=[32, 1], nbb=[32, 32], nrep=32, pc=2, pen=SL, pu=SL,
+         E1=SL, EL=SL, Rm=16, mj=16, mm=2, mp=2, gg=2, wr=SL, whoc=128, ysb=128)
+_declare("sbuf", "bfloat16", fb=32, fr=128, M1=256, C1=256, L1=512, S1=512, trow=SL, tokr=SL, frl=[32, 128], feq=[32, 128],
+         FL=768, FS=768, fb2=64, ft2=64, fr2=SL, M2=512, C2=512, L2=1024, S2=1024)
+_declare("psum", "float32", p0=512, p1=512, p2=512, p3=512, p4=512, p5=512, p6=512, p7=512)
+_DMAS = ["x", "rt", "w", "r2a", "r2b", "vx", "vh", "fd", "fo", "fl", "td", "to", "tl", "wd", "wo", "ti", "wi",
+         "y", "oc", "o0", "o1", "o2", "o3", "who"]
+SEMAPHORES = ["qv", "qa", "qt", "qg", "af", "a1", "at", "a2", "aw", "loc"] + ["d_" + k for k in _DMAS]
+
+
+def plan(T, topo, s):
+    c = T.cores[s]
+    near = [r for r in range(N) if r != s and topo.chip(T.cores[r]) == topo.chip(c)]
+
+    def hops(r):
+        a, b = topo.chip(c), topo.chip(T.cores[r])
+        return 0 if topo.mates(a, b) else 1 if topo.same_plane(a, b) else 2
+    far = sorted([r for r in range(N) if r != s and r not in near], key=lambda r: (hops(r), (r - s) % N))
+    e = topo.engines(c, T.cores[far[0]])
+    k = [x for x in topo.engines(c, T.cores[near[0]]) if x not in e][:2]
+    one = {far[0]: e[0:1], far[1]: e[1:2], far[2]: e[2:3], far[3]: e[3:4], far[4]: e[4:6], far[5]: e[6:8], near[0]: k}
+    two = {far[4]: e[4:5], far[5]: e[5:6], far[0]: e[6:7], far[1]: e[7:8], far[2]: e[0:2], far[3]: e[2:4], near[0]: k}
+    return one, two
+
+
+def rank_program(g, core, T, topo):
+    me = T.rank_of(core)
+    if me is None:
+        return
+    S = T.sem
+    plans = [plan(T, topo, s) for s in range(N)]
+    others = [r for r in range(N) if r != me]
+    eng = {"v": g.vector, "a": g.scalar, "t": g.tensor, "s": g.sync, "g": g}
+    vec = g.vector
+    V = {"set": vec.memset, "copy": vec.tensor_copy, "ts": vec.tensor_scalar, "tt": vec.tensor_tensor,
+         "scan": vec.tensor_tensor_scan, "red": vec.tensor_reduce, "tr": vec.transpose, "qz": vec.quantize_mx}
+    G = {"iota": g.iota, "sel": g.affine_select}
+    cnt = {}
+    seen = {q: {} for q in eng}
+    wr, rd = {}, {}
+
+    def need(q, evs):
+        m = {}
+        for sem, n in evs:
+            m[sem] = max(n, m.get(sem, 0))
+        for sem in sorted(m):
+            if seen[q].get(sem, 0) < m[sem]:
+                eng[q].wait_ge(S[sem], m[sem])
+                seen[q][sem] = m[sem]
+
+    def before(q, reads, writes, part):
+        evs = [e for t in reads for e in wr[t]]
+        if not part:
+            evs += [e for t in writes for e in wr.get(t, []) + rd.get(t, [])]
+        need(q, evs)
+
+    def after(ev, reads, writes, part):
+        for t in reads:
+            rd.setdefault(t, []).append(ev)
+        for t in writes:
+            wr[t] = (wr.get(t, []) if part else []) + [ev]
+            if not part:
+                rd[t] = []
+
+    def op(q, f, args, reads=(), writes=(), part=False, **kw):
+        before(q, reads, writes, part)
+        sem = "q" + q
+        cnt[sem] = cnt.get(sem, 0) + 1
+        f(*args, **kw).then_inc(S[sem], 1)
+        after((sem, cnt[sem]), reads, writes, part)
+
+    def v(name, *args, **kw):
+        op("v", V[name], args, **kw)
+
+    def act(*args, **kw):
+        op("a", g.scalar.activation, args, **kw)
+
+    def mm(*args, **kw):
+        op("t", g.tensor.matmul_mx, args, **kw)
+
+    def gp(name, *args, **kw):
+        op("g", G[name], args, **kw)
+
+    def dma(q, key, out, in_, reads=(), writes=(), part=False):
+        before(q, reads, writes, part)
+        eng[q].dma_start(out, in_).then_inc(S["d_" + key], 16)
+        cnt["d_" + key] = 16
+        after(("d_" + key, 16), reads, writes, part)
+
+    def send(which, sem, src, dst, reads):
+        need("g", [e for t in reads for e in wr[t]])
+        tr = []
+        for d in others:
+            es = plans[me][which][d]
+            rid, pid, _ = topo.addr(T.cores[d])
+            tr.append(RemoteDMATransfer(dst_ids=[DstId(rid=rid, pnc=pid)], dma_engine_mask=sum(1 << e for e in es),
+                                        remote_sem=S[sem], src=src(d), dst=dst(d)))
+            cnt["loc"] = cnt.get("loc", 0) + len(es)
+        g.remote_dma_fused(tr, local_sem=S["loc"])
+
+    def lands(tag, sem, *which):
+        cnt[sem] = sum(len(plans[s][w][me]) for s in others for w in which)
+        wr[tag].append((sem, cnt[sem]))
+
+    u8, u32 = dt.uint8, dt.uint32
+    blk = [slice(32 * b, 32 * b + 32) for b in range(N)]
+
+    dma("s", "x", T.xt[:, 0:512], T.x[:, :], writes=["xt"], part=True)
+    dma("a", "rt", T.rtt[:, 0:4 * N], T.rt[:, 0:4 * N], writes=["rtt"], part=True)
+    dma("s", "w", T.wt[:, :], T.w[:, :], writes=["wt"])
+    if me > 0:
+        dma("a", "r2a", T.r2t[:, 0:4 * me], T.r2[:, 0:4 * me], writes=["r2t"], part=True)
+    dma("a", "r2b", T.r2t[:, 4 * me:4 * N], T.r2[:, 4 * me + 4:4 * N + 4], writes=["r2t"], part=True)
+    dma("s", "vx", T.vxt[:, :], T.vx[:, :], writes=["vxt"])
+    dma("s", "vh", T.vht[:, :], T.vh[:, :], writes=["vht"])
+
+    fl = {"allow_small_or_imprecise_dtypes": True}
+    gp("iota", T.pp[:, :], [[0, 8]], 0, 1, writes=["pp"])
+    gp("iota", T.tokv[:, :], [[1, 144]], 0, 0, writes=["tokv"], **fl)
+    gp("iota", T.cc[:, :], [[1, 8]], 0, 0, writes=["cc"])
+    gp("iota", T.io32[:, :], [[1, 32]], 0, 0, writes=["io32"], **fl)
+    gp("iota", T.base[:, :], [[TK, N], [0, CAPP]], 0, 0, writes=["base"], **fl)
+    v("set", T.rtt[:, 4 * N:512], 0.0, writes=["rtt"], part=True)
+    v("set", T.xt[:, 512:520], 0.0, writes=["xt"], part=True)
+    v("set", T.zb[:, :], 0.0, writes=["zb"])
+    v("set", T.neg8[:, :], -9e29, writes=["neg8"])
+    v("set", T.rsA[:, :], 1.0, writes=["rsA1"])
+    v("ts", T.pb[:, :], T.pp[:, :], 4, 14, A.logical_shift_right, A.bitwise_and, reads=["pp"], writes=["pb"])
+    v("ts", T.p15[:, :], T.pp[:, :], 15, None, A.bitwise_and, reads=["pp"], writes=["p15"])
+    v("set", T.rsA[:, 0:512:128], 0.0, reads=["rsA1"], writes=["rsA"])
+    for u in range(2):
+        v("ts", T.ecol[:, u:u + 1], T.pb[:, 0:1], float(u), None, A.add, reads=["pb"], writes=["ecol"], part=True)
+        v("ts", T.thr1[:, u:u + 1], T.p15[:, 0:1], 16.0 * u, None, A.add, reads=["p15"], writes=["thr1"], part=True)
+    v("set", T.m1[:, :], -1.0, writes=["m1"])
+    dma("a", "wo", T.whol[me:me + 1, 0:CB, 0], T.m1[0:1, 0:CB], reads=["m1"], writes=["whol"], part=True)
+    dma("a", "wi", T.whod[:, :, 0], T.m1[0:N, :], reads=["m1"], writes=["whod"])
+    dma("a", "ti", T.tokd[:, :, 0], T.zb[0:N, :], reads=["zb"], writes=["tokd"])
+    v("set", T.zf[:, :], 0.0, writes=["zf"])
+    gp("sel", T.tri[:, :], T.zf[:, :], [[-1, 128]], A.is_gt, BIG, 0, 1, reads=["zf"], writes=["tri"])
+    v("set", T.rsB[:, :], 1.0, writes=["rsB1"])
+    v("set", T.rsB[:, 0:1024:256], 0.0, reads=["rsB1"], writes=["rsB"])
+
+    v("qz", T.rq[:, :], T.rs[:, :], T.rtt[:, :], reads=["rtt"], writes=["rq"])
+    v("qz", T.xq[:, 0:130], T.xs[:, 0:130], T.xt[:, :], reads=["xt"], writes=["xq"])
+    mm(T.p0[:, 0:128], T.xq[:, 0:128], T.xs[:, 0:128], T.rq[:, :], T.rs[:, :], True, True, reads=["xq", "rq"], writes=["p0"])
+    v("scan", T.R[:, :], T.p0[:, 0:8], T.neg8[:, :], -9e29, A.max, A.max, reads=["p0", "neg8"], writes=["R"])
+    v("ts", T.lt[:, :], T.R[:, :], T.R[:, 7:8], None, A.is_lt, reads=["R"], writes=["lt"])
+    red(v, T.first[:, :], T.lt[:, :], reads=["lt"], writes=["first"])
+    v("ts", T.fb[:, :], T.zb[:, 0:32], T.first[:, 0:1], None, A.add, reads=["zb", "first"], writes=["fb"])
+    dma("s", "fd", T.fd[:, :], T.fb[:, 0:1], reads=["fb"], writes=["fd"])
+    dma("s", "fo", T.fl[me], T.fb[:, 0:1], reads=["fb"], writes=["fl"], part=True)
+    v("tr", T.fr[:, 0:32], T.fb[:, :], reads=["fb"], writes=["frT"])
+    for a in range(1, 4):
+        v("copy", T.fr[0:32, blk[a]], T.fr[blk[a], 0:32], reads=["frT"], writes=["fr"], part=True)
+    v("copy", T.fr[32:64, :], T.fr[0:32, :], reads=["fr", "frT"], writes=["fra"])
+    v("copy", T.fr[64:128, :], T.fr[0:64, :], reads=["fr", "frT", "fra"], writes=["frb"])
+    for u in range(2):
+        v("ts", T.M1[:, 128 * u:128 * u + 128], T.fr[:, :], T.ecol[:, u:u + 1], None, A.is_equal,
+          reads=["fr", "fra", "frb", "ecol"], writes=["M1"], part=True)
+    v("scan", T.C1[:, :], T.rsA[:, 0:256], T.M1[:, :], 0.0, A.mult, A.add, reads=["rsA", "M1"], writes=["C1"])
+    for u in range(2):
+        for h in range(2):
+            k = 128 * (2 * u + h)
+            v("ts", T.L1[:, k:k + 128], T.C1[:, 128 * u:128 * u + 128], T.thr1[:, h:h + 1], None, A.is_le,
+              reads=["C1", "thr1"], writes=["L1"], part=True)
+    v("scan", T.S1[:, :], T.rsA[:, :], T.L1[:, :], 0.0, A.mult, A.add, reads=["rsA", "L1"], writes=["S1"])
+    for b in range(4):
+        v("copy", T.of1[0:32, 4 * b:4 * b + 4], T.S1[blk[b], 127:512:128], reads=["S1"], writes=["of1"], part=True)
+    v("copy", T.off1[0:32, :], T.of1[0:32, :], reads=["of1"], writes=["off1a"], part=True)
+    v("copy", T.off1[32:64, :], T.of1[0:32, :], reads=["of1"], writes=["off1a"], part=True)
+    v("copy", T.off1[64:128, :], T.off1[0:64, :], reads=["off1a"], writes=["off1"])
+    O1 = ["off1a", "off1", "xq"]
+    ms = slice(2 * me, 2 * me + 2)
+    v("copy", T.sq[:, :].bitcast(u32), T.xq[:, 0:130].bitcast(u32).indirect(T.off1[:, :]), reads=O1, writes=["sq"])
+    act(T.ss[:, :], T.xs[:, 0:130].indirect(T.off1[:, :]), F.Copy, reads=O1, writes=["ss"])
+    v("copy", T.xh[:, blk[me]].bitcast(u32), T.xq[:, 0:130].bitcast(u32).indirect(T.off1[:, ms]), reads=O1, writes=["xh"], part=True)
+    act(T.xhs[:, blk[me]], T.xs[:, 0:130].indirect(T.off1[:, ms]), F.Copy, reads=O1, writes=["xh"], part=True)
+    act(T.trow[:, :], T.tokv[:, :].indirect(T.off1[:, :]), F.Copy, reads=O1 + ["tokv"], writes=["trow"])
+
+    send(0, "af", lambda d: T.fd[:, :], lambda d: T.fl[me], ["fd"])
+    send(0, "a1", lambda d: T.sq[:, blk[d]].bitcast(u8), lambda d: T.xh[:, blk[me]].bitcast(u8), ["sq"])
+    send(1, "a1", lambda d: T.ss[:, blk[d]], lambda d: T.xhs[:, blk[me]], ["ss"])
+    dma("s", "td", T.tokd[:, 0:CAPP, 0], T.trow[0:1, :], reads=["trow"], writes=["tokd"])
+    dma("s", "to", T.tokl[me:me + 1, 0:CAPP, 0], T.trow[0:1, blk[me]], reads=["trow"], writes=["tokl"], part=True)
+    send(0, "at", lambda d: T.tokd[d], lambda d: T.tokl[me], ["tokd"])
+
+    for t in range(4):
+        act(T.r8t[:, t:512:4], T.zf[:, :], F.Identity, reads=["r2t", "zf"], writes=["r8t"], part=True, bias=T.r2t[:, 28 + t:29 + t])
+    act(T.rsC[:, :], T.rsB[:, 0:768], F.Identity, reads=["rsB"], writes=["rsC1"], bias=1.0, scale=0.0)
+    act(T.tokw[:, :], T.rsB[:, 0:648], F.Identity, reads=["rsB"], writes=["tokw"], bias=-1.0, scale=0.0)
+    v("qz", T.wq[:, :], T.ws[:, :], T.wt[:, :], reads=["wt"], writes=["wq"])
+    v("set", T.r2t[:, 4 * N:512], 0.0, writes=["r2z"])
+    v("set", T.zt[:, :], 0.0, writes=["zt"])
+    v("set", T.ht[:, 1024:1032], 0.0, writes=["ht"], part=True)
+    v("copy", T.offz[:, :], T.thr1[:, :], reads=["thr1"], writes=["offz"])
+    v("qz", T.xh[:, 256:384], T.xhs[:, 256:384], T.zt[:, :], reads=["zt"], writes=["xhz"])
+    v("qz", T.r2q[:, :], T.r2s[:, :], T.r2t[:, :], reads=["r2t", "r2z"], writes=["r2q"])
+    OZ = ["offz", "xhz"]
+    v("copy", T.l2q[:, blk[me]].bitcast(u32), T.xh[:, 256:384].bitcast(u32).indirect(T.offz[:, :]), reads=OZ, writes=["l2"], part=True)
+    v("copy", T.l2s[:, blk[me]], T.xhs[:, 256:384].indirect(T.offz[:, :]), reads=OZ, writes=["l2"], part=True)
+    v("ts", T.mgt[:, :], T.ecol[:, :], float(me), None, A.is_gt, reads=["ecol"], writes=["mgt"])
+    v("ts", T.p31[:, :], T.pp[:, :], 31, None, A.bitwise_and, reads=["pp"], writes=["p31"])
+    v("ts", T.ia[:, :], T.pp[:, :], 1, 6, A.logical_shift_right, A.bitwise_and, reads=["pp"], writes=["ia"])
+    v("ts", T.ib[:, :], T.pp[:, :], 1, None, A.bitwise_and, reads=["pp"], writes=["ib"])
+    v("ts", T.px[:, :], T.pp[:, :], 1, 1, A.logical_shift_right, A.bitwise_and, reads=["pp"], writes=["px"])
+    v("ts", T.ie[:, :], T.pp[:, :], 14, None, A.bitwise_and, reads=["pp"], writes=["ie"])
+    v("ts", T.ig[:, :], T.cc[:, :], 32.0, 2.0, A.mult, A.add, reads=["cc"], writes=["ig"])
+    v("tt", T.mcol[:, :], T.ecol[:, :], T.mgt[:, :], A.subtract, reads=["ecol", "mgt"], writes=["mcol"])
+    v("copy", T.ccol[:, :], T.p31[:, 0:1], reads=["p31"], writes=["ccol"])
+    v("tt", T.ic[:, :], T.ia[:, :], T.ib[:, :], A.add, reads=["ia", "ib"], writes=["ic"])
+    v("ts", T.xadd[:, :], T.px[:, 0:1], float(HO), None, A.mult, reads=["px"], writes=["xadd"])
+    v("ts", T.ie[:, :], T.ie[:, :], 2.0, None, A.mult, reads=["ie"], writes=["ie"])
+    v("tt", T.ig[:, :], T.ig[:, :], T.ib[:, :], A.add, reads=["ig", "ib"], writes=["ig"])
+    for h in range(2):
+        v("ts", T.thr2[:, h:h + 1], T.ic[:, 0:1], 8.0 * h, None, A.add, reads=["ic"], writes=["thr2"], part=True)
+    v("tt", T.ig[:, :], T.ig[:, :], T.ie[:, :], A.add, reads=["ie", "ig"], writes=["ig"])
+    v("set", T.nb[:, :], 0.0, writes=["nb"])
+    v("copy", T.offh[:, :], T.ig[:, :], reads=["ig"], writes=["offh"])
+    v("qz", T.r8q[:, :], T.r8s[:, :], T.r8t[:, :], reads=["r8t"], writes=["r8q"])
+    v("set", T.rsC[:, 0:768:384], 0.0, reads=["rsC1"], writes=["rsC"])
+
+    lands("fl", "af", 0)
+    dma("s", "fl", T.frl[0:8, :], T.fl[:, :, 0], reads=["fl"], writes=["frl"])
+    v("ts", T.feq[0:8, :], T.frl[0:8, :], float(me), None, A.is_equal, reads=["frl"], writes=["feq"])
+    red(v, T.nb[0:8, :], T.feq[0:8, :], reads=["feq"], writes=["nb"])
+    v("ts", T.nbb[:, :], T.zb[0:32, 0:32], T.nb[:, 0:1], None, A.add, reads=["zb", "nb"], writes=["nbb"])
+    v("tr", T.nrep[0:32, :], T.nbb[:, :], reads=["nbb"], writes=["nrep"])
+    v("copy", T.nrep[32:64, :], T.nrep[0:32, :], reads=["nrep"], writes=["nrep1"])
+    v("copy", T.nrep[64:128, :], T.nrep[0:64, :], reads=["nrep", "nrep1"], writes=["nrep2"])
+    NR = ["nrep", "nrep1", "nrep2"]
+    for s in range(N):
+        v("ts", T.pen[:, blk[s]], T.io32[:, :], T.nrep[:, s:s + 1], BIG, A.is_ge, A.mult, reads=NR + ["io32"], writes=["pen"], part=True)
+    for a in range(4):
+        v("ts", T.pc[blk[a], :], T.nrep[blk[a], a:8:4], T.ccol[blk[a], 0:1], OUT, A.is_le, A.mult,
+          reads=NR + ["ccol"], writes=["pc"], part=True)
+    for h in range(2):
+        k = slice(128 * h, 128 * h + 128)
+        v("tt", T.pu[:, k], T.pen[:, k], T.tri[:, :], A.add, reads=["pen", "tri"], writes=["pu"], part=True)
+
+    lands("xh", "a1", 0, 1)
+    P, PE = [T.p1, T.p2, T.p3, T.p4], [T.p6, T.p7]
+    for i in range(4):
+        k = slice(128 * i, 128 * i + 128)
+        mm(P[i][:, 0:SL], T.wq[:, k], T.ws[:, k], T.xh[:, 0:SL], T.xhs[:, 0:SL], True, True, reads=["wq", "xh"], writes=["pw%d" % i])
+    for i in range(4):
+        if i % 2:
+            v("ts", T.ht[:, i:1024:4], P[i][:, 0:SL], 0.0, 0.0625, A.max, A.mult, reads=["pw%d" % i], writes=["ht"], part=True)
+        else:
+            act(T.ht[:, i:1024:4], P[i][:, 0:SL], F.Relu, reads=["pw%d" % i], writes=["ht"], part=True, scale=0.0625)
+    v("qz", T.xh[:, HO:XW], T.xhs[:, HO:XW], T.ht[:, :], reads=["ht"], writes=["h"])
+    mm(T.p5[:, 0:SL], T.r8q[:, :], T.r8s[:, :], T.xh[:, HO:HO + SL], T.xhs[:, HO:HO + SL], True, True, reads=["r8q", "h"], writes=["per"])
+    for h in range(2):
+        k = slice(HO + 128 * h, HO + 128 * h + 128)
+        mm(PE[h][:, 0:128], T.xh[:, k], T.xhs[:, k], T.r2q[:, :], T.r2s[:, :], True, True, reads=["r2q", "h"], writes=["pe%d" % h])
+    v("tt", T.E1[:, :], T.p5[:, 0:SL], T.pen[:, :], A.add, reads=["per", "pen"], writes=["E1"])
+    v("tt", T.EL[:, :], T.p5[:, 0:SL], T.pu[:, :], A.add, reads=["per", "pu"], writes=["EL"])
+    for h in range(2):
+        k = 8 * h
+        v("scan", T.Rm[:, k:k + 7], PE[h][:, 0:7], T.neg8[:, 0:7], -9e29, A.max, A.max, reads=["pe%d" % h, "neg8"], writes=["Rm%d" % h])
+        act(T.mj[:, k:k + 7], T.Rm[:, k:k + 7], F.Sign, reads=["Rm%d" % h], writes=["mm"], part=True,
+            bias=T.Rm[:, k + 6:k + 7], scale=-1.0, accum_out=T.mm[:, h:h + 1])
+    for h in range(2):
+        k = 384 * h
+        e8 = PE[h][:, 7:8]
+        if h:
+            v("ts", T.FL[:, k:k + 128], T.E1[:, 0:128], e8, None, A.is_le, reads=["E1", "pe1"], writes=["FL"], part=True)
+        v("ts", T.FL[:, k + 128 * h:k + 256], T.E1[:, 128 * h:256], e8, None, A.is_lt, reads=["E1", "pe%d" % h], writes=["FL"], part=True)
+        v("ts", T.FL[:, k + 256:k + 384], T.EL[:, 128 * h:128 * h + 128], e8, None, A.is_equal,
+          reads=["EL", "pe%d" % h], writes=["FL"], part=True)
+    v("scan", T.FS[:, :], T.rsC[:, :], T.FL[:, :], 0.0, A.mult, A.add, reads=["rsC", "FL"], writes=["FS"])
+    v("tt", T.mp[:, :], T.mm[:, :], T.pc[:, :], A.add, reads=["mm", "pc"], writes=["mp"])
+    v("ts", T.gg[:, :], T.FS[:, 383:768:384], float(DF), OUT, A.is_ge, A.mult, reads=["FS"], writes=["gg"])
+    for h in range(2):
+        v("ts", T.fb2[:, blk[h]], T.zb[:, 0:32], T.gg[:, h:h + 1], T.mp[:, h:h + 1], A.add, A.add,
+          reads=["zb", "gg", "mp"], writes=["fb2"], part=True)
+    v("tr", T.ft2[:, :], T.fb2[:, :], reads=["fb2"], writes=["ft2"])
+    for h in range(2):
+        for a in range(4):
+            v("copy", T.fr2[0:32, blk[4 * h + a]], T.ft2[blk[a], blk[h]], reads=["ft2"], writes=["fr2"], part=True)
+    v("copy", T.fr2[32:64, :], T.fr2[0:32, :], reads=["fr2"], writes=["fr2a"])
+    v("copy", T.fr2[64:128, :], T.fr2[0:64, :], reads=["fr2", "fr2a"], writes=["fr2b"])
+    for u in range(2):
+        v("ts", T.M2[:, 256 * u:256 * u + 256], T.fr2[:, :], T.mcol[:, u:u + 1], None, A.is_equal,
+          reads=["fr2", "fr2a", "fr2b", "mcol"], writes=["M2"], part=True)
+    v("scan", T.C2[:, :], T.rsB[:, 0:512], T.M2[:, :], 0.0, A.mult, A.add, reads=["rsB", "M2"], writes=["C2"])
+    for u in range(2):
+        for h in range(2):
+            k = 256 * (2 * u + h)
+            v("ts", T.L2[:, k:k + 256], T.C2[:, 256 * u:256 * u + 256], T.thr2[:, h:h + 1], None, A.is_le,
+              reads=["C2", "thr2"], writes=["L2"], part=True)
+    v("scan", T.S2[:, :], T.rsB[:, :], T.L2[:, :], 0.0, A.mult, A.add, reads=["rsB", "L2"], writes=["S2"])
+    for b in range(4):
+        v("copy", T.of2[0:32, 4 * b:4 * b + 4], T.S2[blk[b], 255:1024:256], reads=["S2"], writes=["of2"], part=True)
+    for k in range(2):
+        v("ts", T.off2[blk[k], :], T.of2[0:32, :], T.xadd[0:32, 0:1], None, A.add, reads=["of2", "xadd"], writes=["off2a"], part=True)
+    v("copy", T.off2[64:128, :], T.off2[0:64, :], reads=["off2a"], writes=["off2"])
+    O2 = ["off2a", "off2"]
+    XR = O2 + ["xh", "xhz", "h"]
+    v("copy", T.s2q[:, :].bitcast(u32), T.xh[:, 0:XW].bitcast(u32).indirect(T.off2[:, :]), reads=XR, writes=["s2q"])
+    act(T.s2s[:, :], T.xhs[:, 0:XW].indirect(T.off2[:, :]), F.Copy, reads=XR, writes=["s2s"])
+    send(0, "a2", lambda d: T.s2q[:, blk[d]].bitcast(u8), lambda d: T.l2q[:, blk[me]].bitcast(u8), ["s2q"])
+    send(1, "a2", lambda d: T.s2s[:, blk[d]], lambda d: T.l2s[:, blk[me]], ["s2s"])
+
+    v("qz", T.vxq[:, :], T.vxs[:, :], T.vxt[:, :], reads=["vxt"], writes=["vxq"])
+    v("qz", T.vhq[:, :], T.vhs[:, :], T.vht[:, :], reads=["vht"], writes=["vhq"])
+    lands("tokl", "at", 0)
+    dma("s", "tl", T.tokr[0:1, :], T.tokl[:, 0:CAPP, 0], reads=["tokl"], writes=["tokr"])
+    v("tt", T.tokw[0:1, 0:SL], T.tokr[0:1, :], T.base[0:1, :], A.add, reads=["tokr", "base"], writes=["tokw"])
+    act(T.wr[:, :], T.tokw[:, :].indirect(T.off2[:, :]), F.Copy, reads=O2 + ["tokw"], writes=["wr"])
+    for k in range(2):
+        v("copy", T.whoc[0:1, k:128:2], T.wr[0:1, k:SL:4], reads=["wr"], writes=["whoc"], part=True)
+    dma("s", "wd", T.whod[:, 0:CB, 0], T.whoc[0:1, :], reads=["whoc"], writes=["whod"])
+    send(0, "aw", lambda d: T.whod[d], lambda d: T.whol[me], ["whod"])
+
+    lands("l2", "a2", 0, 1)
+    mm(T.p0[:, 0:254], T.vxq[:, :], T.vxs[:, :], T.l2q[:, 0:254], T.l2s[:, 0:254], True, False, reads=["vxq", "l2"], writes=["p0"])
+    mm(T.p0[:, 0:254], T.vhq[:, :], T.vhs[:, :], T.l2q[:, 2:256], T.l2s[:, 2:256], False, True, reads=["vhq", "l2"], writes=["p0"], part=True)
+    v("copy", T.hq[:, :].bitcast(u32), T.l2q[:, :].bitcast(u32).indirect(T.offh[:, :]), reads=["l2", "offh"], writes=["hq"])
+    act(T.hs[:, :], T.l2s[:, :].indirect(T.offh[:, :]), F.Copy, reads=["l2", "offh"], writes=["hs"])
+    for k in range(2):
+        v("copy", T.ysb[:, k:128:2], T.p0[:, k:254:4], reads=["p0"], writes=["ysb"], part=True)
+    dma("s", "oc", T.oc[:, :], T.hq[:, :].bitcast(u8), reads=["hq"], writes=["oc"])
+    for k in range(4):
+        dma("a", "o%d" % k, T.osc[4 * k:4 * k + 4, :], T.hs[32 * k:32 * k + 4, :], reads=["hs"], writes=["osc%d" % k])
+    dma("s", "y", T.y[:, :], T.ysb[:, :], reads=["ysb"], writes=["y"])
+    lands("whol", "aw", 0)
+    dma("s", "who", T.who[0:1, :], T.whol[:, 0:CB, 0], reads=["whol"], writes=["who"])
+    need("g", sorted(cnt.items()))
+
+
+def red(v, out, in_, **kw):
+    v("red", out, in_, axis=AxisListType.X, op=A.add, **kw)

@@ -25,14 +25,14 @@ _declare("sbuf", "float8_e4m3fn_x4", xq=136, rq=128, wq=512, r2q=128, r8q=128, v
 _declare("sbuf", "uint8", xs=136, rs=128, ws=512, r2s=128, r8s=128, vxs=128, vhs=128, ss=SL, xhs=648, s2s=SL, l2s=SL, hs=128)
 _declare("dram", "bfloat16", fd=[128, 1], fl=[N, 128, 1], tokd=[N, 128, 1], tokl=[N, 128, 1])
 _declare("dram", "float32", whod=[N, 128, 1], whol=[N, 128, 1])
-_declare("sbuf", "int32", pp=8, cc=8, ia=8, ib=8, ic=8, ie=8, ig=8, p15=8, p31=8, px=8, pb=8)
-_declare("sbuf", "float32", thr1=2, thr2=2, xadd=1, ccol=1, ecol=2, mcol=2, mgt=2, neg8=8, zf=128, tri=128, io32=32, base=SL, m1=128)
-_declare("sbuf", "bfloat16", zb=128, rsA=512, rsB=1024, rsC=768, tokv=144)
+_declare("sbuf", "int32", pp=8, cc=8, ig=8, ih=8, p15=8, p31=8, pb=8)
+_declare("sbuf", "float32", thr1=2, ccol=1, ecol=2, mcol=2, mgt=2, neg8=8, zf=128, io32=32, m1=128)
+_declare("sbuf", "bfloat16", zb=128, rsA=512, rsB=512, rsC=384, tokv=144)
 _declare("sbuf", "uint16", offz=2, offh=8, off1=16, off2=16)
-_declare("sbuf", "float32", R=8, lt=8, first=1, of1=16, of2=16, tokw=648, nb=[32, 1], nbb=[32, 32], nrep=32, pc=2, pen=SL, pu=SL,
-         E1=SL, EL=SL, Rm=16, mj=16, mm=2, mp=2, gg=2, wr=SL, whoc=128, ysb=128)
+_declare("sbuf", "float32", R=8, lt=8, first=1, tokw=648, nb=[32, 1], nbb=[32, 32], nrep=32, pc=2, pen=SL, pu=SL,
+         E1=SL, EL=SL, Rm=16, mj=16, mm=2, mp=2, rk=1, gg=2, wr=SL, ysb=128)
 _declare("sbuf", "bfloat16", fb=32, fr=128, M1=256, C1=256, L1=512, S1=512, trow=SL, tokr=SL, frl=[32, 128], feq=[32, 128],
-         FL=768, FS=768, fb2=64, ft2=64, fr2=SL, M2=512, C2=512, L2=1024, S2=1024)
+         FL=768, FS=384, FJ=384, fb2=64, ft2=64, fr2=SL, M2=512, C2=512, L2=512, S2=512)
 _declare("psum", "float32", p0=512, p1=512, p2=512, p3=512, p4=512, p5=512, p6=512, p7=512)
 _DMAS = ["x", "rt", "w", "r2a", "r2b", "vx", "vh", "fd", "fo", "fl", "td", "to", "tl", "wd", "wo", "ti", "wi",
          "y", "oc", "o0", "o1", "o2", "o3", "who"]
@@ -51,7 +51,7 @@ def plan(T, topo, s):
     k = [x for x in topo.engines(c, T.cores[near[0]]) if x not in e][:2]
     one = {far[0]: e[0:1], far[1]: e[1:2], far[2]: e[2:3], far[3]: e[3:4], far[4]: e[4:6], far[5]: e[6:8], near[0]: k}
     two = {far[4]: e[4:5], far[5]: e[5:6], far[0]: e[6:7], far[1]: e[7:8], far[2]: e[0:2], far[3]: e[2:4], near[0]: k}
-    return one, two
+    return one, two, {**one, near[0]: e}
 
 
 def rank_program(g, core, T, topo):
@@ -61,6 +61,8 @@ def rank_program(g, core, T, topo):
     S = T.sem
     plans = [plan(T, topo, s) for s in range(N)]
     others = [r for r in range(N) if r != me]
+    far = [r for r in others if topo.chip(T.cores[r]) != topo.chip(core)]
+    near = [r for r in others if r not in far]
     eng = {"v": g.vector, "a": g.scalar, "t": g.tensor, "s": g.sync, "g": g}
     vec = g.vector
     V = {"set": vec.memset, "copy": vec.tensor_copy, "ts": vec.tensor_scalar, "tt": vec.tensor_tensor,
@@ -118,10 +120,10 @@ def rank_program(g, core, T, topo):
         cnt["d_" + key] = 16
         after(("d_" + key, 16), reads, writes, part)
 
-    def send(which, sem, src, dst, reads):
+    def send(to, which, sem, src, dst, reads):
         need("g", [e for t in reads for e in wr[t]])
         tr = []
-        for d in others:
+        for d in to:
             es = plans[me][which][d]
             rid, pid, _ = topo.addr(T.cores[d])
             tr.append(RemoteDMATransfer(dst_ids=[DstId(rid=rid, pnc=pid)], dma_engine_mask=sum(1 << e for e in es),
@@ -142,15 +144,15 @@ def rank_program(g, core, T, topo):
     if me > 0:
         dma("a", "r2a", T.r2t[:, 0:4 * me], T.r2[:, 0:4 * me], writes=["r2t"], part=True)
     dma("a", "r2b", T.r2t[:, 4 * me:4 * N], T.r2[:, 4 * me + 4:4 * N + 4], writes=["r2t"], part=True)
-    dma("s", "vx", T.vxt[:, :], T.vx[:, :], writes=["vxt"])
-    dma("s", "vh", T.vht[:, :], T.vh[:, :], writes=["vht"])
 
     fl = {"allow_small_or_imprecise_dtypes": True}
     gp("iota", T.pp[:, :], [[0, 8]], 0, 1, writes=["pp"])
+    gp("iota", T.m1[:, :], [[0, 128]], -1, 0, writes=["m1"], **fl)
     gp("iota", T.tokv[:, :], [[1, 144]], 0, 0, writes=["tokv"], **fl)
     gp("iota", T.cc[:, :], [[1, 8]], 0, 0, writes=["cc"])
+    gp("iota", T.zf[:, :], [[0, 128]], 0, 0, writes=["zf"], **fl)
     gp("iota", T.io32[:, :], [[1, 32]], 0, 0, writes=["io32"], **fl)
-    gp("iota", T.base[:, :], [[TK, N], [0, CAPP]], 0, 0, writes=["base"], **fl)
+    gp("iota", T.zt[:, :], [[0, 512]], 0, 0, writes=["zt"], **fl)
     v("set", T.rtt[:, 4 * N:512], 0.0, writes=["rtt"], part=True)
     v("set", T.xt[:, 512:520], 0.0, writes=["xt"], part=True)
     v("set", T.zb[:, :], 0.0, writes=["zb"])
@@ -162,14 +164,9 @@ def rank_program(g, core, T, topo):
     for u in range(2):
         v("ts", T.ecol[:, u:u + 1], T.pb[:, 0:1], float(u), None, A.add, reads=["pb"], writes=["ecol"], part=True)
         v("ts", T.thr1[:, u:u + 1], T.p15[:, 0:1], 16.0 * u, None, A.add, reads=["p15"], writes=["thr1"], part=True)
-    v("set", T.m1[:, :], -1.0, writes=["m1"])
     dma("a", "wo", T.whol[me:me + 1, 0:CB, 0], T.m1[0:1, 0:CB], reads=["m1"], writes=["whol"], part=True)
     dma("a", "wi", T.whod[:, :, 0], T.m1[0:N, :], reads=["m1"], writes=["whod"])
     dma("a", "ti", T.tokd[:, :, 0], T.zb[0:N, :], reads=["zb"], writes=["tokd"])
-    v("set", T.zf[:, :], 0.0, writes=["zf"])
-    gp("sel", T.tri[:, :], T.zf[:, :], [[-1, 128]], A.is_gt, BIG, 0, 1, reads=["zf"], writes=["tri"])
-    v("set", T.rsB[:, :], 1.0, writes=["rsB1"])
-    v("set", T.rsB[:, 0:1024:256], 0.0, reads=["rsB1"], writes=["rsB"])
 
     v("qz", T.rq[:, :], T.rs[:, :], T.rtt[:, :], reads=["rtt"], writes=["rq"])
     v("qz", T.xq[:, 0:130], T.xs[:, 0:130], T.xt[:, :], reads=["xt"], writes=["xq"])
@@ -180,6 +177,7 @@ def rank_program(g, core, T, topo):
     v("ts", T.fb[:, :], T.zb[:, 0:32], T.first[:, 0:1], None, A.add, reads=["zb", "first"], writes=["fb"])
     dma("s", "fd", T.fd[:, :], T.fb[:, 0:1], reads=["fb"], writes=["fd"])
     dma("s", "fo", T.fl[me], T.fb[:, 0:1], reads=["fb"], writes=["fl"], part=True)
+    send(near, 2, "af", lambda d: T.fb[:, 0:1], lambda d: T.fl[me], ["fb"])
     v("tr", T.fr[:, 0:32], T.fb[:, :], reads=["fb"], writes=["frT"])
     for a in range(1, 4):
         v("copy", T.fr[0:32, blk[a]], T.fr[blk[a], 0:32], reads=["frT"], writes=["fr"], part=True)
@@ -196,11 +194,10 @@ def rank_program(g, core, T, topo):
               reads=["C1", "thr1"], writes=["L1"], part=True)
     v("scan", T.S1[:, :], T.rsA[:, :], T.L1[:, :], 0.0, A.mult, A.add, reads=["rsA", "L1"], writes=["S1"])
     for b in range(4):
-        v("copy", T.of1[0:32, 4 * b:4 * b + 4], T.S1[blk[b], 127:512:128], reads=["S1"], writes=["of1"], part=True)
-    v("copy", T.off1[0:32, :], T.of1[0:32, :], reads=["of1"], writes=["off1a"], part=True)
-    v("copy", T.off1[32:64, :], T.of1[0:32, :], reads=["of1"], writes=["off1a"], part=True)
-    v("copy", T.off1[64:128, :], T.off1[0:64, :], reads=["off1a"], writes=["off1"])
-    O1 = ["off1a", "off1", "xq"]
+        v("ts", T.off1[0:32, 4 * b:4 * b + 4], T.S1[blk[b], 127:512:128], 0.0, None, A.add, reads=["S1"], writes=["off1"], part=True)
+    v("copy", T.off1[32:64, :], T.off1[0:32, :], reads=["off1"], writes=["off1a"])
+    v("copy", T.off1[64:128, :], T.off1[0:64, :], reads=["off1", "off1a"], writes=["off1b"])
+    O1 = ["off1", "off1a", "off1b", "xq"]
     ms = slice(2 * me, 2 * me + 2)
     v("copy", T.sq[:, :].bitcast(u32), T.xq[:, 0:130].bitcast(u32).indirect(T.off1[:, :]), reads=O1, writes=["sq"])
     act(T.ss[:, :], T.xs[:, 0:130].indirect(T.off1[:, :]), F.Copy, reads=O1, writes=["ss"])
@@ -208,21 +205,21 @@ def rank_program(g, core, T, topo):
     act(T.xhs[:, blk[me]], T.xs[:, 0:130].indirect(T.off1[:, ms]), F.Copy, reads=O1, writes=["xh"], part=True)
     act(T.trow[:, :], T.tokv[:, :].indirect(T.off1[:, :]), F.Copy, reads=O1 + ["tokv"], writes=["trow"])
 
-    send(0, "af", lambda d: T.fd[:, :], lambda d: T.fl[me], ["fd"])
-    send(0, "a1", lambda d: T.sq[:, blk[d]].bitcast(u8), lambda d: T.xh[:, blk[me]].bitcast(u8), ["sq"])
-    send(1, "a1", lambda d: T.ss[:, blk[d]], lambda d: T.xhs[:, blk[me]], ["ss"])
+    send(far, 2, "af", lambda d: T.fd[:, :], lambda d: T.fl[me], ["fd"])
+    send(others, 0, "a1", lambda d: T.sq[:, blk[d]].bitcast(u8), lambda d: T.xh[:, blk[me]].bitcast(u8), ["sq"])
+    send(others, 1, "a1", lambda d: T.ss[:, blk[d]], lambda d: T.xhs[:, blk[me]], ["ss"])
     dma("s", "td", T.tokd[:, 0:CAPP, 0], T.trow[0:1, :], reads=["trow"], writes=["tokd"])
     dma("s", "to", T.tokl[me:me + 1, 0:CAPP, 0], T.trow[0:1, blk[me]], reads=["trow"], writes=["tokl"], part=True)
-    send(0, "at", lambda d: T.tokd[d], lambda d: T.tokl[me], ["tokd"])
+    send(others, 0, "at", lambda d: T.tokd[d], lambda d: T.tokl[me], ["tokd"])
 
     for t in range(4):
         act(T.r8t[:, t:512:4], T.zf[:, :], F.Identity, reads=["r2t", "zf"], writes=["r8t"], part=True, bias=T.r2t[:, 28 + t:29 + t])
-    act(T.rsC[:, :], T.rsB[:, 0:768], F.Identity, reads=["rsB"], writes=["rsC1"], bias=1.0, scale=0.0)
-    act(T.tokw[:, :], T.rsB[:, 0:648], F.Identity, reads=["rsB"], writes=["tokw"], bias=-1.0, scale=0.0)
+    act(T.rsC[:, :], T.wt[:, 0:384], F.Identity, reads=["wt"], writes=["rsC"], bias=1.0, scale=0.0)
+    act(T.rsB[:, :], T.wt[:, 0:512], F.Identity, reads=["wt"], writes=["rsB1"], bias=1.0, scale=0.0)
+    act(T.tokw[:, :], T.wt[:, 0:648], F.Identity, reads=["wt"], writes=["tokw"], bias=-1.0, scale=0.0)
     v("qz", T.wq[:, :], T.ws[:, :], T.wt[:, :], reads=["wt"], writes=["wq"])
     v("set", T.r2t[:, 4 * N:512], 0.0, writes=["r2z"])
-    v("set", T.zt[:, :], 0.0, writes=["zt"])
-    v("set", T.ht[:, 1024:1032], 0.0, writes=["ht"], part=True)
+    v("set", T.ht[:, 1024:1032], 0.0, writes=["htz"])
     v("copy", T.offz[:, :], T.thr1[:, :], reads=["thr1"], writes=["offz"])
     v("qz", T.xh[:, 256:384], T.xhs[:, 256:384], T.zt[:, :], reads=["zt"], writes=["xhz"])
     v("qz", T.r2q[:, :], T.r2s[:, :], T.r2t[:, :], reads=["r2t", "r2z"], writes=["r2q"])
@@ -231,26 +228,16 @@ def rank_program(g, core, T, topo):
     v("copy", T.l2s[:, blk[me]], T.xhs[:, 256:384].indirect(T.offz[:, :]), reads=OZ, writes=["l2"], part=True)
     v("ts", T.mgt[:, :], T.ecol[:, :], float(me), None, A.is_gt, reads=["ecol"], writes=["mgt"])
     v("ts", T.p31[:, :], T.pp[:, :], 31, None, A.bitwise_and, reads=["pp"], writes=["p31"])
-    v("ts", T.ia[:, :], T.pp[:, :], 1, 6, A.logical_shift_right, A.bitwise_and, reads=["pp"], writes=["ia"])
-    v("ts", T.ib[:, :], T.pp[:, :], 1, None, A.bitwise_and, reads=["pp"], writes=["ib"])
-    v("ts", T.px[:, :], T.pp[:, :], 1, 1, A.logical_shift_right, A.bitwise_and, reads=["pp"], writes=["px"])
-    v("ts", T.ie[:, :], T.pp[:, :], 14, None, A.bitwise_and, reads=["pp"], writes=["ie"])
-    v("ts", T.ig[:, :], T.cc[:, :], 32.0, 2.0, A.mult, A.add, reads=["cc"], writes=["ig"])
+    v("ts", T.ig[:, :], T.cc[:, :], 32.0, float(CB), A.mult, A.add, reads=["cc"], writes=["ig"])
+    v("set", T.nb[:, :], 0.0, writes=["nb"])
     v("tt", T.mcol[:, :], T.ecol[:, :], T.mgt[:, :], A.subtract, reads=["ecol", "mgt"], writes=["mcol"])
     v("copy", T.ccol[:, :], T.p31[:, 0:1], reads=["p31"], writes=["ccol"])
-    v("tt", T.ic[:, :], T.ia[:, :], T.ib[:, :], A.add, reads=["ia", "ib"], writes=["ic"])
-    v("ts", T.xadd[:, :], T.px[:, 0:1], float(HO), None, A.mult, reads=["px"], writes=["xadd"])
-    v("ts", T.ie[:, :], T.ie[:, :], 2.0, None, A.mult, reads=["ie"], writes=["ie"])
-    v("tt", T.ig[:, :], T.ig[:, :], T.ib[:, :], A.add, reads=["ig", "ib"], writes=["ig"])
-    for h in range(2):
-        v("ts", T.thr2[:, h:h + 1], T.ic[:, 0:1], 8.0 * h, None, A.add, reads=["ic"], writes=["thr2"], part=True)
-    v("tt", T.ig[:, :], T.ig[:, :], T.ie[:, :], A.add, reads=["ie", "ig"], writes=["ig"])
-    v("set", T.nb[:, :], 0.0, writes=["nb"])
-    v("copy", T.offh[:, :], T.ig[:, :], reads=["ig"], writes=["offh"])
+    v("tt", T.ih[:, :], T.ig[:, :], T.p15[:, :], A.add, reads=["ig", "p15"], writes=["ih"])
     v("qz", T.r8q[:, :], T.r8s[:, :], T.r8t[:, :], reads=["r8t"], writes=["r8q"])
-    v("set", T.rsC[:, 0:768:384], 0.0, reads=["rsC1"], writes=["rsC"])
+    v("copy", T.offh[:, :], T.ih[:, :], reads=["ih"], writes=["offh"])
+    v("set", T.rsB[:, 0:512:256], 0.0, reads=["rsB1"], writes=["rsB"])
 
-    lands("fl", "af", 0)
+    lands("fl", "af", 2)
     dma("s", "fl", T.frl[0:8, :], T.fl[:, :, 0], reads=["fl"], writes=["frl"])
     v("ts", T.feq[0:8, :], T.frl[0:8, :], float(me), None, A.is_equal, reads=["frl"], writes=["feq"])
     red(v, T.nb[0:8, :], T.feq[0:8, :], reads=["feq"], writes=["nb"])
@@ -261,46 +248,69 @@ def rank_program(g, core, T, topo):
     NR = ["nrep", "nrep1", "nrep2"]
     for s in range(N):
         v("ts", T.pen[:, blk[s]], T.io32[:, :], T.nrep[:, s:s + 1], BIG, A.is_ge, A.mult, reads=NR + ["io32"], writes=["pen"], part=True)
+    for h in range(2):
+        k = slice(128 * h, 128 * h + 128)
+        gp("sel", T.pu[:, k], T.pen[:, k], [[-1, 128]], A.is_gt, BIG, 0, 1, reads=["pen"], writes=["pu"], part=True)
     for a in range(4):
         v("ts", T.pc[blk[a], :], T.nrep[blk[a], a:8:4], T.ccol[blk[a], 0:1], OUT, A.is_le, A.mult,
           reads=NR + ["ccol"], writes=["pc"], part=True)
-    for h in range(2):
-        k = slice(128 * h, 128 * h + 128)
-        v("tt", T.pu[:, k], T.pen[:, k], T.tri[:, :], A.add, reads=["pen", "tri"], writes=["pu"], part=True)
+    lands("tokl", "at", 0)
+    dma("s", "tl", T.tokr[0:1, :], T.tokl[:, 0:CAPP, 0], reads=["tokl"], writes=["tokr"])
+    dma("s", "vx", T.vxt[:, :], T.vx[:, :], writes=["vxt"])
+    dma("s", "vh", T.vht[:, :], T.vh[:, :], writes=["vht"])
 
     lands("xh", "a1", 0, 1)
-    P, PE = [T.p1, T.p2, T.p3, T.p4], [T.p6, T.p7]
-    for i in range(4):
-        k = slice(128 * i, 128 * i + 128)
-        mm(P[i][:, 0:SL], T.wq[:, k], T.ws[:, k], T.xh[:, 0:SL], T.xhs[:, 0:SL], True, True, reads=["wq", "xh"], writes=["pw%d" % i])
-    for i in range(4):
-        if i % 2:
-            v("ts", T.ht[:, i:1024:4], P[i][:, 0:SL], 0.0, 0.0625, A.max, A.mult, reads=["pw%d" % i], writes=["ht"], part=True)
-        else:
-            act(T.ht[:, i:1024:4], P[i][:, 0:SL], F.Relu, reads=["pw%d" % i], writes=["ht"], part=True, scale=0.0625)
-    v("qz", T.xh[:, HO:XW], T.xhs[:, HO:XW], T.ht[:, :], reads=["ht"], writes=["h"])
-    mm(T.p5[:, 0:SL], T.r8q[:, :], T.r8s[:, :], T.xh[:, HO:HO + SL], T.xhs[:, HO:HO + SL], True, True, reads=["r8q", "h"], writes=["per"])
+    P = [[T.p1, T.p2, T.p3, T.p4], [T.p0, T.p5, T.p6, T.p7]]
+    B = [["p1", "p2", "p3", "p4"], ["p0", "p5", "p6", "p7"]]
     for h in range(2):
+        k = slice(128 * h, 128 * h + 128)
+        for i in range(4):
+            j = slice(128 * i, 128 * i + 128)
+            mm(P[h][i][:, 0:128], T.wq[:, j], T.ws[:, j], T.xh[:, k], T.xhs[:, k], True, True, reads=["wq", "xh"], writes=[B[h][i]])
+    for h in range(2):
+        e = 512 * (h + 1)
+        for i in range(4):
+            o = T.ht[:, 512 * h + i:e:4]
+            if i % 2:
+                v("ts", o, P[h][i][:, 0:128], 0.0, 0.0625, A.max, A.mult, reads=[B[h][i]], writes=["ht%d" % h], part=True)
+            else:
+                act(o, P[h][i][:, 0:128], F.Relu, reads=[B[h][i]], writes=["ht%d" % h], part=True, scale=0.0625)
+        k = slice(HO + 128 * h, XW if h else HO + 128)
+        v("qz", T.xh[:, k], T.xhs[:, k], T.ht[:, 512 * h:e + 8 * h], reads=["ht%d" % h, "htz"], writes=["h%d" % h])
+    ROW, PE, pe = T.p1, [T.p2, T.p3], ["p2", "p3"]
+    H = ["h0", "h1"]
+
+    def columns(h):
         k = slice(HO + 128 * h, HO + 128 * h + 128)
-        mm(PE[h][:, 0:128], T.xh[:, k], T.xhs[:, k], T.r2q[:, :], T.r2s[:, :], True, True, reads=["r2q", "h"], writes=["pe%d" % h])
-    v("tt", T.E1[:, :], T.p5[:, 0:SL], T.pen[:, :], A.add, reads=["per", "pen"], writes=["E1"])
-    v("tt", T.EL[:, :], T.p5[:, 0:SL], T.pu[:, :], A.add, reads=["per", "pu"], writes=["EL"])
-    for h in range(2):
+        mm(PE[h][:, 0:128], T.xh[:, k], T.xhs[:, k], T.r2q[:, :], T.r2s[:, :], True, True, reads=["r2q", H[h]], writes=[pe[h]])
+    columns(0)
+    mm(ROW[:, 0:SL], T.r8q[:, :], T.r8s[:, :], T.xh[:, HO:HO + SL], T.xhs[:, HO:HO + SL], True, True, reads=["r8q"] + H, writes=["p1"])
+    columns(1)
+
+    def second(h):
         k = 8 * h
-        v("scan", T.Rm[:, k:k + 7], PE[h][:, 0:7], T.neg8[:, 0:7], -9e29, A.max, A.max, reads=["pe%d" % h, "neg8"], writes=["Rm%d" % h])
+        v("scan", T.Rm[:, k:k + 7], PE[h][:, 0:7], T.neg8[:, 0:7], -9e29, A.max, A.max, reads=[pe[h], "neg8"], writes=["Rm%d" % h])
         act(T.mj[:, k:k + 7], T.Rm[:, k:k + 7], F.Sign, reads=["Rm%d" % h], writes=["mm"], part=True,
             bias=T.Rm[:, k + 6:k + 7], scale=-1.0, accum_out=T.mm[:, h:h + 1])
+    second(0)
+    v("tt", T.E1[:, :], ROW[:, 0:SL], T.pen[:, :], A.add, reads=["p1", "pen"], writes=["E1"])
+    v("tt", T.EL[:, :], ROW[:, 0:SL], T.pu[:, :], A.add, reads=["p1", "pu"], writes=["EL"])
+    second(1)
     for h in range(2):
         k = 384 * h
-        e8 = PE[h][:, 7:8]
+        e8, t = PE[h][:, 7:8], "FL%d" % h
         if h:
-            v("ts", T.FL[:, k:k + 128], T.E1[:, 0:128], e8, None, A.is_le, reads=["E1", "pe1"], writes=["FL"], part=True)
-        v("ts", T.FL[:, k + 128 * h:k + 256], T.E1[:, 128 * h:256], e8, None, A.is_lt, reads=["E1", "pe%d" % h], writes=["FL"], part=True)
-        v("ts", T.FL[:, k + 256:k + 384], T.EL[:, 128 * h:128 * h + 128], e8, None, A.is_equal,
-          reads=["EL", "pe%d" % h], writes=["FL"], part=True)
-    v("scan", T.FS[:, :], T.rsC[:, :], T.FL[:, :], 0.0, A.mult, A.add, reads=["rsC", "FL"], writes=["FS"])
+            v("ts", T.FL[:, k:k + 128], T.E1[:, 0:128], e8, None, A.is_le, reads=["E1", pe[h]], writes=[t], part=True)
+        v("ts", T.FL[:, k + 128 * h:k + 256], T.E1[:, 128 * h:256], e8, None, A.is_lt, reads=["E1", pe[h]], writes=[t], part=True)
+        v("ts", T.FL[:, k + 256:k + 384], T.EL[:, 128 * h:128 * h + 128], e8, None, A.is_equal, reads=["EL", pe[h]], writes=[t], part=True)
+        if h == 0:
+            act(T.FJ[:, :], T.FL[:, 0:384], F.Identity, reads=[t], writes=["rk"], accum_out=T.rk[:, 0:1])
+    v("scan", T.FS[:, :], T.rsC[:, :], T.FL[:, 384:768], 0.0, A.mult, A.add, reads=["rsC", "FL1"], writes=["FS"])
+    for s in range(N):
+        act(T.tokw[0:1, blk[s]], T.tokr[0:1, blk[s]], F.Identity, reads=["tokr"], writes=["tokw"], part=True, bias=float(s * TK))
     v("tt", T.mp[:, :], T.mm[:, :], T.pc[:, :], A.add, reads=["mm", "pc"], writes=["mp"])
-    v("ts", T.gg[:, :], T.FS[:, 383:768:384], float(DF), OUT, A.is_ge, A.mult, reads=["FS"], writes=["gg"])
+    v("ts", T.gg[:, 0:1], T.rk[:, 0:1], float(DF), OUT, A.is_ge, A.mult, reads=["rk"], writes=["gg"], part=True)
+    v("ts", T.gg[:, 1:2], T.FS[:, 383:384], float(DF), OUT, A.is_ge, A.mult, reads=["FS"], writes=["gg"], part=True)
     for h in range(2):
         v("ts", T.fb2[:, blk[h]], T.zb[:, 0:32], T.gg[:, h:h + 1], T.mp[:, h:h + 1], A.add, A.add,
           reads=["zb", "gg", "mp"], writes=["fb2"], part=True)
@@ -313,50 +323,47 @@ def rank_program(g, core, T, topo):
     for u in range(2):
         v("ts", T.M2[:, 256 * u:256 * u + 256], T.fr2[:, :], T.mcol[:, u:u + 1], None, A.is_equal,
           reads=["fr2", "fr2a", "fr2b", "mcol"], writes=["M2"], part=True)
-    v("scan", T.C2[:, :], T.rsB[:, 0:512], T.M2[:, :], 0.0, A.mult, A.add, reads=["rsB", "M2"], writes=["C2"])
-    for u in range(2):
-        for h in range(2):
-            k = 256 * (2 * u + h)
-            v("ts", T.L2[:, k:k + 256], T.C2[:, 256 * u:256 * u + 256], T.thr2[:, h:h + 1], None, A.is_le,
-              reads=["C2", "thr2"], writes=["L2"], part=True)
+    v("scan", T.C2[:, :], T.rsB[:, :], T.M2[:, :], 0.0, A.mult, A.add, reads=["rsB", "M2"], writes=["C2"])
+    v("ts", T.L2[:, :], T.C2[:, :], T.thr1[:, 0:1], None, A.is_le, reads=["C2", "thr1"], writes=["L2"])
     v("scan", T.S2[:, :], T.rsB[:, :], T.L2[:, :], 0.0, A.mult, A.add, reads=["rsB", "L2"], writes=["S2"])
     for b in range(4):
-        v("copy", T.of2[0:32, 4 * b:4 * b + 4], T.S2[blk[b], 255:1024:256], reads=["S2"], writes=["of2"], part=True)
-    for k in range(2):
-        v("ts", T.off2[blk[k], :], T.of2[0:32, :], T.xadd[0:32, 0:1], None, A.add, reads=["of2", "xadd"], writes=["off2a"], part=True)
-    v("copy", T.off2[64:128, :], T.off2[0:64, :], reads=["off2a"], writes=["off2"])
-    O2 = ["off2a", "off2"]
-    XR = O2 + ["xh", "xhz", "h"]
+        v("ts", T.off2[0:32, 4 * b:4 * b + 4:2], T.S2[blk[b], 255:512:256], 0.0, None, A.add, reads=["S2"], writes=["off2"], part=True)
+    v("ts", T.off2[0:32, 1:16:2], T.off2[0:32, 0:16:2], float(HO), None, A.add, reads=["off2"], writes=["off2h"])
+    v("copy", T.off2[32:64, :], T.off2[0:32, :], reads=["off2", "off2h"], writes=["off2a"])
+    v("copy", T.off2[64:128, :], T.off2[0:64, :], reads=["off2", "off2h", "off2a"], writes=["off2b"])
+    O2 = ["off2", "off2h", "off2a", "off2b"]
+    XR = O2 + ["xh", "xhz", "h0", "h1"]
     v("copy", T.s2q[:, :].bitcast(u32), T.xh[:, 0:XW].bitcast(u32).indirect(T.off2[:, :]), reads=XR, writes=["s2q"])
     act(T.s2s[:, :], T.xhs[:, 0:XW].indirect(T.off2[:, :]), F.Copy, reads=XR, writes=["s2s"])
-    send(0, "a2", lambda d: T.s2q[:, blk[d]].bitcast(u8), lambda d: T.l2q[:, blk[me]].bitcast(u8), ["s2q"])
-    send(1, "a2", lambda d: T.s2s[:, blk[d]], lambda d: T.l2s[:, blk[me]], ["s2s"])
+    send(others, 0, "a2", lambda d: T.s2q[:, blk[d]].bitcast(u8), lambda d: T.l2q[:, blk[me]].bitcast(u8), ["s2q"])
+    send(others, 1, "a2", lambda d: T.s2s[:, blk[d]], lambda d: T.l2s[:, blk[me]], ["s2s"])
 
+    act(T.wr[:, :], T.tokw[:, :].indirect(T.off2[:, :]), F.Copy, reads=O2 + ["tokw"], writes=["wr"])
+    dma("s", "wd", T.whod[:, 0:2 * CB, 0], T.wr[0:1, :], reads=["wr"], writes=["whod"])
+    send(others, 0, "aw", lambda d: T.whod[d], lambda d: T.whol[me], ["whod"])
     v("qz", T.vxq[:, :], T.vxs[:, :], T.vxt[:, :], reads=["vxt"], writes=["vxq"])
     v("qz", T.vhq[:, :], T.vhs[:, :], T.vht[:, :], reads=["vht"], writes=["vhq"])
-    lands("tokl", "at", 0)
-    dma("s", "tl", T.tokr[0:1, :], T.tokl[:, 0:CAPP, 0], reads=["tokl"], writes=["tokr"])
-    v("tt", T.tokw[0:1, 0:SL], T.tokr[0:1, :], T.base[0:1, :], A.add, reads=["tokr", "base"], writes=["tokw"])
-    act(T.wr[:, :], T.tokw[:, :].indirect(T.off2[:, :]), F.Copy, reads=O2 + ["tokw"], writes=["wr"])
-    for k in range(2):
-        v("copy", T.whoc[0:1, k:128:2], T.wr[0:1, k:SL:4], reads=["wr"], writes=["whoc"], part=True)
-    dma("s", "wd", T.whod[:, 0:CB, 0], T.whoc[0:1, :], reads=["whoc"], writes=["whod"])
-    send(0, "aw", lambda d: T.whod[d], lambda d: T.whol[me], ["whod"])
 
     lands("l2", "a2", 0, 1)
-    mm(T.p0[:, 0:254], T.vxq[:, :], T.vxs[:, :], T.l2q[:, 0:254], T.l2s[:, 0:254], True, False, reads=["vxq", "l2"], writes=["p0"])
-    mm(T.p0[:, 0:254], T.vhq[:, :], T.vhs[:, :], T.l2q[:, 2:256], T.l2s[:, 2:256], False, True, reads=["vhq", "l2"], writes=["p0"], part=True)
+    Y = [T.p0, T.p5]
+    for q in range(2):
+        k, j, t = slice(112 * q, 112 * q + 128), slice(112 * q + CB, 112 * q + CB + 128), ["p0", "p5"][q]
+        mm(Y[q][:, 0:128], T.vxq[:, :], T.vxs[:, :], T.l2q[:, k], T.l2s[:, k], True, False, reads=["vxq", "l2"], writes=[t])
+        mm(Y[q][:, 0:128], T.vhq[:, :], T.vhs[:, :], T.l2q[:, j], T.l2s[:, j], False, True, reads=["vhq", "l2"], writes=[t], part=True)
     v("copy", T.hq[:, :].bitcast(u32), T.l2q[:, :].bitcast(u32).indirect(T.offh[:, :]), reads=["l2", "offh"], writes=["hq"])
     act(T.hs[:, :], T.l2s[:, :].indirect(T.offh[:, :]), F.Copy, reads=["l2", "offh"], writes=["hs"])
-    for k in range(2):
-        v("copy", T.ysb[:, k:128:2], T.p0[:, k:254:4], reads=["p0"], writes=["ysb"], part=True)
+    for a in range(N):
+        k = 32 * a - 112 * (a // 4)
+        v("copy", T.ysb[:, CB * a:CB * a + CB], Y[a // 4][:, k:k + CB], reads=[["p0", "p5"][a // 4]], writes=["ysb"], part=True)
     dma("s", "oc", T.oc[:, :], T.hq[:, :].bitcast(u8), reads=["hq"], writes=["oc"])
     for k in range(4):
         dma("a", "o%d" % k, T.osc[4 * k:4 * k + 4, :], T.hs[32 * k:32 * k + 4, :], reads=["hs"], writes=["osc%d" % k])
     dma("s", "y", T.y[:, :], T.ysb[:, :], reads=["ysb"], writes=["y"])
     lands("whol", "aw", 0)
     dma("s", "who", T.who[0:1, :], T.whol[:, 0:CB, 0], reads=["whol"], writes=["who"])
-    need("g", sorted(cnt.items()))
+    for sem in sorted(cnt):
+        if max(seen[q].get(sem, 0) for q in eng) < cnt[sem]:
+            need("a" if sem[:3] == "d_o" and sem != "d_oc" else "s" if sem[:2] == "d_" else "g", [(sem, cnt[sem])])
 
 
 def red(v, out, in_, **kw):

@@ -10,7 +10,7 @@ SL = N * CAPP
 HO = 384
 XW = 642
 BIG = 1e29
-OUT = 100.0
+OUT = 200.0
 
 SCRATCH = {}
 
@@ -26,13 +26,13 @@ _declare("sbuf", "uint8", xs=136, rs=128, ws=512, r2s=128, r8s=128, vxs=128, vhs
 _declare("dram", "bfloat16", fd=[128, 1], fl=[N, 128, 1], tokd=[N, 128, 1], tokl=[N, 128, 1])
 _declare("dram", "float32", whod=[N, 128, 1], whol=[N, 128, 1])
 _declare("sbuf", "int32", pp=8, cc=8, ig=8, ih=8, p15=8, p31=8, pb=8)
-_declare("sbuf", "float32", thr1=2, ccol=1, ecol=2, mcol=2, mgt=2, neg8=8, zf=128, io32=32, m1=128)
-_declare("sbuf", "bfloat16", zb=128, rsA=512, rsB=512, rsC=384, tokv=144)
+_declare("sbuf", "float32", thr1=2, ccol=1, ecol=2, mgt=2, mct=2, mcol=2, neg8=8, io32=32, m1=128)
+_declare("sbuf", "bfloat16", zb=128, rsA=512, c128=32, one=2 * SL, sgn=2 * SL, soff=SL, tokv=144)
 _declare("sbuf", "uint16", offz=2, offh=8, off1=16, off2=16)
-_declare("sbuf", "float32", R=8, lt=8, first=1, tokw=648, nb=[32, 1], nbb=[32, 32], nrep=32, pc=2, pen=SL, pu=SL,
-         E1=SL, EL=SL, Rm=16, mj=16, mm=2, mp=2, rk=1, gg=2, wr=SL, ysb=128)
+_declare("sbuf", "float32", R=8, lt=8, first=1, nb=[32, 1], nbb=[32, 32], nrep=32, pc=2, pen=SL,
+         E1=SL, eb=2, Rm=16, mj=16, mm=2, sg=2, tokw=648, wr=SL, ysb=128)
 _declare("sbuf", "bfloat16", fb=32, fr=128, M1=256, C1=256, L1=512, S1=512, trow=SL, tokr=SL, frl=[32, 128], feq=[32, 128],
-         FL=768, FS=384, FJ=384, fb2=64, ft2=64, fr2=SL, M2=512, C2=512, L2=512, S2=512)
+         EQ=2 * SL, FS=2 * SL, SJ=2 * SL, mp=2, fb2=64, ft2=[128, 2, 32], fr2=[128, 2, 128], M2=2 * SL, C2=2 * SL, L2=2 * SL, S2=2 * SL)
 _declare("psum", "float32", p0=512, p1=512, p2=512, p3=512, p4=512, p5=512, p6=512, p7=512)
 _DMAS = ["x", "rt", "w", "r2a", "r2b", "vx", "vh", "fd", "fo", "fl", "td", "to", "tl", "wd", "wo", "ti", "wi",
          "y", "oc", "o0", "o1", "o2", "o3", "who"]
@@ -137,6 +137,8 @@ def rank_program(g, core, T, topo):
 
     u8, u32 = dt.uint8, dt.uint32
     blk = [slice(32 * b, 32 * b + 32) for b in range(N)]
+    half = [slice(128 * h, 128 * h + 128) for h in range(4)]
+    row = [slice(SL * h, SL * h + SL) for h in range(2)]
 
     dma("s", "x", T.xt[:, 0:512], T.x[:, :], writes=["xt"], part=True)
     dma("a", "rt", T.rtt[:, 0:4 * N], T.rt[:, 0:4 * N], writes=["rtt"], part=True)
@@ -147,23 +149,22 @@ def rank_program(g, core, T, topo):
 
     fl = {"allow_small_or_imprecise_dtypes": True}
     gp("iota", T.pp[:, :], [[0, 8]], 0, 1, writes=["pp"])
-    gp("iota", T.m1[:, :], [[0, 128]], -1, 0, writes=["m1"], **fl)
     gp("iota", T.tokv[:, :], [[1, 144]], 0, 0, writes=["tokv"], **fl)
+    gp("iota", T.m1[:, :], [[0, 128]], -1, 0, writes=["m1"], **fl)
     gp("iota", T.cc[:, :], [[1, 8]], 0, 0, writes=["cc"])
-    gp("iota", T.zf[:, :], [[0, 128]], 0, 0, writes=["zf"], **fl)
     gp("iota", T.io32[:, :], [[1, 32]], 0, 0, writes=["io32"], **fl)
-    gp("iota", T.zt[:, :], [[0, 512]], 0, 0, writes=["zt"], **fl)
+    v("set", T.zb[:, :], 0.0, writes=["zb"])
     v("set", T.rtt[:, 4 * N:512], 0.0, writes=["rtt"], part=True)
     v("set", T.xt[:, 512:520], 0.0, writes=["xt"], part=True)
-    v("set", T.zb[:, :], 0.0, writes=["zb"])
     v("set", T.neg8[:, :], -9e29, writes=["neg8"])
-    v("set", T.rsA[:, :], 1.0, writes=["rsA1"])
     v("ts", T.pb[:, :], T.pp[:, :], 4, 14, A.logical_shift_right, A.bitwise_and, reads=["pp"], writes=["pb"])
     v("ts", T.p15[:, :], T.pp[:, :], 15, None, A.bitwise_and, reads=["pp"], writes=["p15"])
-    v("set", T.rsA[:, 0:512:128], 0.0, reads=["rsA1"], writes=["rsA"])
     for u in range(2):
         v("ts", T.ecol[:, u:u + 1], T.pb[:, 0:1], float(u), None, A.add, reads=["pb"], writes=["ecol"], part=True)
         v("ts", T.thr1[:, u:u + 1], T.p15[:, 0:1], 16.0 * u, None, A.add, reads=["p15"], writes=["thr1"], part=True)
+    for k in range(4):
+        act(T.rsA[:, half[k]], T.zb[:, :], F.Identity, reads=["zb"], writes=["rsA1"], part=True, bias=1.0)
+    act(T.rsA[:, 0:512:128], T.zb[:, 0:4], F.Copy, reads=["zb", "rsA1"], writes=["rsA"])
     dma("a", "wo", T.whol[me:me + 1, 0:CB, 0], T.m1[0:1, 0:CB], reads=["m1"], writes=["whol"], part=True)
     dma("a", "wi", T.whod[:, :, 0], T.m1[0:N, :], reads=["m1"], writes=["whod"])
     dma("a", "ti", T.tokd[:, :, 0], T.zb[0:N, :], reads=["zb"], writes=["tokd"])
@@ -181,23 +182,22 @@ def rank_program(g, core, T, topo):
     v("tr", T.fr[:, 0:32], T.fb[:, :], reads=["fb"], writes=["frT"])
     for a in range(1, 4):
         v("copy", T.fr[0:32, blk[a]], T.fr[blk[a], 0:32], reads=["frT"], writes=["fr"], part=True)
-    v("copy", T.fr[32:64, :], T.fr[0:32, :], reads=["fr", "frT"], writes=["fra"])
-    v("copy", T.fr[64:128, :], T.fr[0:64, :], reads=["fr", "frT", "fra"], writes=["frb"])
+    for b in range(1, 4):
+        v("copy", T.fr[blk[b], :], T.fr[0:32, :], reads=["fr", "frT"], writes=["fra"], part=b > 1)
     for u in range(2):
-        v("ts", T.M1[:, 128 * u:128 * u + 128], T.fr[:, :], T.ecol[:, u:u + 1], None, A.is_equal,
-          reads=["fr", "fra", "frb", "ecol"], writes=["M1"], part=True)
+        v("ts", T.M1[:, half[u]], T.fr[:, :], T.ecol[:, u:u + 1], None, A.is_equal,
+          reads=["fr", "fra", "ecol"], writes=["M1"], part=True)
     v("scan", T.C1[:, :], T.rsA[:, 0:256], T.M1[:, :], 0.0, A.mult, A.add, reads=["rsA", "M1"], writes=["C1"])
     for u in range(2):
         for h in range(2):
-            k = 128 * (2 * u + h)
-            v("ts", T.L1[:, k:k + 128], T.C1[:, 128 * u:128 * u + 128], T.thr1[:, h:h + 1], None, A.is_le,
+            v("ts", T.L1[:, half[2 * u + h]], T.C1[:, half[u]], T.thr1[:, h:h + 1], None, A.is_le,
               reads=["C1", "thr1"], writes=["L1"], part=True)
     v("scan", T.S1[:, :], T.rsA[:, :], T.L1[:, :], 0.0, A.mult, A.add, reads=["rsA", "L1"], writes=["S1"])
     for b in range(4):
         v("ts", T.off1[0:32, 4 * b:4 * b + 4], T.S1[blk[b], 127:512:128], 0.0, None, A.add, reads=["S1"], writes=["off1"], part=True)
-    v("copy", T.off1[32:64, :], T.off1[0:32, :], reads=["off1"], writes=["off1a"])
-    v("copy", T.off1[64:128, :], T.off1[0:64, :], reads=["off1", "off1a"], writes=["off1b"])
-    O1 = ["off1", "off1a", "off1b", "xq"]
+    for b in range(1, 4):
+        v("copy", T.off1[blk[b], :], T.off1[0:32, :], reads=["off1"], writes=["off1a"], part=True)
+    O1 = ["off1", "off1a", "xq"]
     ms = slice(2 * me, 2 * me + 2)
     v("copy", T.sq[:, :].bitcast(u32), T.xq[:, 0:130].bitcast(u32).indirect(T.off1[:, :]), reads=O1, writes=["sq"])
     act(T.ss[:, :], T.xs[:, 0:130].indirect(T.off1[:, :]), F.Copy, reads=O1, writes=["ss"])
@@ -208,52 +208,63 @@ def rank_program(g, core, T, topo):
     send(far, 2, "af", lambda d: T.fd[:, :], lambda d: T.fl[me], ["fd"])
     send(others, 0, "a1", lambda d: T.sq[:, blk[d]].bitcast(u8), lambda d: T.xh[:, blk[me]].bitcast(u8), ["sq"])
     send(others, 1, "a1", lambda d: T.ss[:, blk[d]], lambda d: T.xhs[:, blk[me]], ["ss"])
+    lands("fl", "af", 2)
+    dma("s", "fl", T.frl[0:8, :], T.fl[:, :, 0], reads=["fl"], writes=["frl"])
     dma("s", "td", T.tokd[:, 0:CAPP, 0], T.trow[0:1, :], reads=["trow"], writes=["tokd"])
     dma("s", "to", T.tokl[me:me + 1, 0:CAPP, 0], T.trow[0:1, blk[me]], reads=["trow"], writes=["tokl"], part=True)
-    send(others, 0, "at", lambda d: T.tokd[d], lambda d: T.tokl[me], ["tokd"])
 
+    act(T.sgn[:, :], T.wt[:, 0:2 * SL], F.Identity, reads=["wt"], writes=["sgn1"], bias=1.0, scale=0.0)
     for t in range(4):
-        act(T.r8t[:, t:512:4], T.zf[:, :], F.Identity, reads=["r2t", "zf"], writes=["r8t"], part=True, bias=T.r2t[:, 28 + t:29 + t])
-    act(T.rsC[:, :], T.wt[:, 0:384], F.Identity, reads=["wt"], writes=["rsC"], bias=1.0, scale=0.0)
-    act(T.rsB[:, :], T.wt[:, 0:512], F.Identity, reads=["wt"], writes=["rsB1"], bias=1.0, scale=0.0)
-    act(T.tokw[:, :], T.wt[:, 0:648], F.Identity, reads=["wt"], writes=["tokw"], bias=-1.0, scale=0.0)
+        act(T.r8t[:, t:512:4], T.zb[:, :], F.Identity, reads=["r2t", "zb"], writes=["r8t"], part=True, bias=T.r2t[:, 28 + t:29 + t])
+    act(T.one[:, :], T.wt[:, 0:2 * SL], F.Identity, reads=["wt"], writes=["one1"], bias=1.0, scale=0.0)
+    act(T.tokw[:, :], T.wt[:, 0:648], F.Identity, reads=["wt"], writes=["tokm"], bias=-1.0, scale=0.0)
     v("qz", T.wq[:, :], T.ws[:, :], T.wt[:, :], reads=["wt"], writes=["wq"])
+    v("set", T.zt[:, :], 0.0, writes=["zt"])
     v("set", T.r2t[:, 4 * N:512], 0.0, writes=["r2z"])
     v("set", T.ht[:, 1024:1032], 0.0, writes=["htz"])
     v("copy", T.offz[:, :], T.thr1[:, :], reads=["thr1"], writes=["offz"])
     v("qz", T.xh[:, 256:384], T.xhs[:, 256:384], T.zt[:, :], reads=["zt"], writes=["xhz"])
     v("qz", T.r2q[:, :], T.r2s[:, :], T.r2t[:, :], reads=["r2t", "r2z"], writes=["r2q"])
+    v("ts", T.p31[:, :], T.pp[:, :], 31, None, A.bitwise_and, reads=["pp"], writes=["p31"])
+    v("set", T.nb[:, :], 0.0, writes=["nb"])
+    v("qz", T.r8q[:, :], T.r8s[:, :], T.r8t[:, :], reads=["r8t"], writes=["r8q"])
+    v("copy", T.ccol[:, :], T.p31[:, 0:1], reads=["p31"], writes=["ccol"])
     OZ = ["offz", "xhz"]
     v("copy", T.l2q[:, blk[me]].bitcast(u32), T.xh[:, 256:384].bitcast(u32).indirect(T.offz[:, :]), reads=OZ, writes=["l2"], part=True)
     v("copy", T.l2s[:, blk[me]], T.xhs[:, 256:384].indirect(T.offz[:, :]), reads=OZ, writes=["l2"], part=True)
-    v("ts", T.mgt[:, :], T.ecol[:, :], float(me), None, A.is_gt, reads=["ecol"], writes=["mgt"])
-    v("ts", T.p31[:, :], T.pp[:, :], 31, None, A.bitwise_and, reads=["pp"], writes=["p31"])
     v("ts", T.ig[:, :], T.cc[:, :], 32.0, float(CB), A.mult, A.add, reads=["cc"], writes=["ig"])
-    v("set", T.nb[:, :], 0.0, writes=["nb"])
-    v("tt", T.mcol[:, :], T.ecol[:, :], T.mgt[:, :], A.subtract, reads=["ecol", "mgt"], writes=["mcol"])
-    v("copy", T.ccol[:, :], T.p31[:, 0:1], reads=["p31"], writes=["ccol"])
+    v("ts", T.mgt[:, :], T.ecol[:, :], float(me), -1.0, A.is_gt, A.mult, reads=["ecol"], writes=["mgt"])
     v("tt", T.ih[:, :], T.ig[:, :], T.p15[:, :], A.add, reads=["ig", "p15"], writes=["ih"])
-    v("qz", T.r8q[:, :], T.r8s[:, :], T.r8t[:, :], reads=["r8t"], writes=["r8q"])
+    v("tt", T.mct[:, :], T.ecol[:, :], T.mgt[:, :], A.add, reads=["ecol", "mgt"], writes=["mct"])
     v("copy", T.offh[:, :], T.ih[:, :], reads=["ih"], writes=["offh"])
-    v("set", T.rsB[:, 0:512:256], 0.0, reads=["rsB1"], writes=["rsB"])
+    v("ts", T.mcol[:, :], T.mct[:, :], 2.0, None, A.mult, reads=["mct"], writes=["mcol"])
+    v("set", T.c128[:, :], 128.0, writes=["c128"])
+    v("set", T.one[:, 0:2 * SL:SL], 0.0, reads=["one1"], writes=["one"])
+    for h in range(2):
+        k = slice(SL * h + 128 * h, SL * h + 128 * h + 128)
+        gp("sel", T.sgn[:, k], T.sgn[:, k], [[-1, 128]], A.not_equal, -1.0, 0, 1, reads=["sgn1"], writes=["sgn"], part=True)
+    gp("iota", T.soff[:, :], [[TK, N], [0, CAPP]], 0, 0, writes=["soff"], **fl)
+    send(others, 0, "at", lambda d: T.tokd[d], lambda d: T.tokl[me], ["tokd"])
 
-    lands("fl", "af", 2)
-    dma("s", "fl", T.frl[0:8, :], T.fl[:, :, 0], reads=["fl"], writes=["frl"])
     v("ts", T.feq[0:8, :], T.frl[0:8, :], float(me), None, A.is_equal, reads=["frl"], writes=["feq"])
     red(v, T.nb[0:8, :], T.feq[0:8, :], reads=["feq"], writes=["nb"])
     v("ts", T.nbb[:, :], T.zb[0:32, 0:32], T.nb[:, 0:1], None, A.add, reads=["zb", "nb"], writes=["nbb"])
     v("tr", T.nrep[0:32, :], T.nbb[:, :], reads=["nbb"], writes=["nrep"])
-    v("copy", T.nrep[32:64, :], T.nrep[0:32, :], reads=["nrep"], writes=["nrep1"])
-    v("copy", T.nrep[64:128, :], T.nrep[0:64, :], reads=["nrep", "nrep1"], writes=["nrep2"])
-    NR = ["nrep", "nrep1", "nrep2"]
-    for s in range(N):
-        v("ts", T.pen[:, blk[s]], T.io32[:, :], T.nrep[:, s:s + 1], BIG, A.is_ge, A.mult, reads=NR + ["io32"], writes=["pen"], part=True)
-    for h in range(2):
-        k = slice(128 * h, 128 * h + 128)
-        gp("sel", T.pu[:, k], T.pen[:, k], [[-1, 128]], A.is_gt, BIG, 0, 1, reads=["pen"], writes=["pu"], part=True)
-    for a in range(4):
-        v("ts", T.pc[blk[a], :], T.nrep[blk[a], a:8:4], T.ccol[blk[a], 0:1], OUT, A.is_le, A.mult,
-          reads=NR + ["ccol"], writes=["pc"], part=True)
+    for b in range(1, 4):
+        v("copy", T.nrep[blk[b], :], T.nrep[0:32, :], reads=["nrep"], writes=["nrepa"], part=True)
+    NR = ["nrep", "nrepa"]
+
+    def pens(*ranks):
+        for s in ranks:
+            v("ts", T.pen[:, blk[s]], T.io32[:, :], T.nrep[:, s:s + 1], BIG, A.is_ge, A.mult,
+              reads=NR + ["io32"], writes=["pen%d" % (s // 4)], part=True)
+
+    def pcs(*blocks):
+        for a in blocks:
+            v("ts", T.pc[blk[a], :], T.nrep[blk[a], a:8:4], T.ccol[blk[a], 0:1], OUT, A.is_le, A.mult,
+              reads=NR + ["ccol"], writes=["pc"], part=True)
+    fill = {(0, 1): [(pens, 0, 1)], (0, 3): [(pens, 2, 3)], (0, 4): [(pens, 4, 5)],
+            (1, 1): [(pens, 6, 7)], (1, 3): [(pcs, 0, 1)], (1, 4): [(pcs, 2, 3)]}
     lands("tokl", "at", 0)
     dma("s", "tl", T.tokr[0:1, :], T.tokl[:, 0:CAPP, 0], reads=["tokl"], writes=["tokr"])
     dma("s", "vx", T.vxt[:, :], T.vx[:, :], writes=["vxt"])
@@ -263,102 +274,110 @@ def rank_program(g, core, T, topo):
     P = [[T.p1, T.p2, T.p3, T.p4], [T.p0, T.p5, T.p6, T.p7]]
     B = [["p1", "p2", "p3", "p4"], ["p0", "p5", "p6", "p7"]]
     for h in range(2):
-        k = slice(128 * h, 128 * h + 128)
         for i in range(4):
-            j = slice(128 * i, 128 * i + 128)
-            mm(P[h][i][:, 0:128], T.wq[:, j], T.ws[:, j], T.xh[:, k], T.xhs[:, k], True, True, reads=["wq", "xh"], writes=[B[h][i]])
+            mm(P[h][i][:, 0:128], T.wq[:, half[i]], T.ws[:, half[i]], T.xh[:, half[h]], T.xhs[:, half[h]], True, True,
+               reads=["wq", "xh"], writes=[B[h][i]])
+    ROW, rw, PE, pe = [T.p1, T.p4], ["p1", "p4"], [T.p2, T.p3], ["p2", "p3"]
+
+    def products(h):
+        k = slice(HO + 128 * h, HO + 128 * h + 128)
+        mm(ROW[h][:, 0:128], T.r8q[:, :], T.r8s[:, :], T.xh[:, k], T.xhs[:, k], True, True, reads=["r8q", "h%d" % h], writes=[rw[h]])
+        mm(PE[h][:, 0:128], T.xh[:, k], T.xhs[:, k], T.r2q[:, :], T.r2s[:, :], True, True, reads=["r2q", "h%d" % h], writes=[pe[h]])
     for h in range(2):
         e = 512 * (h + 1)
         for i in range(4):
             o = T.ht[:, 512 * h + i:e:4]
             if i % 2:
                 v("ts", o, P[h][i][:, 0:128], 0.0, 0.0625, A.max, A.mult, reads=[B[h][i]], writes=["ht%d" % h], part=True)
+                for f, *n in fill.get((h, i), []):
+                    f(*n)
             else:
                 act(o, P[h][i][:, 0:128], F.Relu, reads=[B[h][i]], writes=["ht%d" % h], part=True, scale=0.0625)
         k = slice(HO + 128 * h, XW if h else HO + 128)
         v("qz", T.xh[:, k], T.xhs[:, k], T.ht[:, 512 * h:e + 8 * h], reads=["ht%d" % h, "htz"], writes=["h%d" % h])
-    ROW, PE, pe = T.p1, [T.p2, T.p3], ["p2", "p3"]
-    H = ["h0", "h1"]
-
-    def columns(h):
-        k = slice(HO + 128 * h, HO + 128 * h + 128)
-        mm(PE[h][:, 0:128], T.xh[:, k], T.xhs[:, k], T.r2q[:, :], T.r2s[:, :], True, True, reads=["r2q", H[h]], writes=[pe[h]])
-    columns(0)
-    mm(ROW[:, 0:SL], T.r8q[:, :], T.r8s[:, :], T.xh[:, HO:HO + SL], T.xhs[:, HO:HO + SL], True, True, reads=["r8q"] + H, writes=["p1"])
-    columns(1)
+        products(h)
+        for f, *n in fill.get((h, 4), []):
+            f(*n)
 
     def second(h):
         k = 8 * h
+        v("copy", T.eb[:, h:h + 1], PE[h][:, 7:8], reads=[pe[h]], writes=["eb%d" % h])
         v("scan", T.Rm[:, k:k + 7], PE[h][:, 0:7], T.neg8[:, 0:7], -9e29, A.max, A.max, reads=[pe[h], "neg8"], writes=["Rm%d" % h])
-        act(T.mj[:, k:k + 7], T.Rm[:, k:k + 7], F.Sign, reads=["Rm%d" % h], writes=["mm"], part=True,
-            bias=T.Rm[:, k + 6:k + 7], scale=-1.0, accum_out=T.mm[:, h:h + 1])
+
+    def away(h):
+        v("tt", T.E1[:, half[h]], ROW[h][:, 0:128], T.pen[:, half[h]], A.add, reads=[rw[h], "pen%d" % h], writes=["E1"], part=True)
     second(0)
-    v("tt", T.E1[:, :], ROW[:, 0:SL], T.pen[:, :], A.add, reads=["p1", "pen"], writes=["E1"])
-    v("tt", T.EL[:, :], ROW[:, 0:SL], T.pu[:, :], A.add, reads=["p1", "pu"], writes=["EL"])
+    away(0)
+    away(1)
     second(1)
     for h in range(2):
-        k = 384 * h
-        e8, t = PE[h][:, 7:8], "FL%d" % h
-        if h:
-            v("ts", T.FL[:, k:k + 128], T.E1[:, 0:128], e8, None, A.is_le, reads=["E1", pe[h]], writes=[t], part=True)
-        v("ts", T.FL[:, k + 128 * h:k + 256], T.E1[:, 128 * h:256], e8, None, A.is_lt, reads=["E1", pe[h]], writes=[t], part=True)
-        v("ts", T.FL[:, k + 256:k + 384], T.EL[:, 128 * h:128 * h + 128], e8, None, A.is_equal, reads=["EL", pe[h]], writes=[t], part=True)
-        if h == 0:
-            act(T.FJ[:, :], T.FL[:, 0:384], F.Identity, reads=[t], writes=["rk"], accum_out=T.rk[:, 0:1])
-    v("scan", T.FS[:, :], T.rsC[:, :], T.FL[:, 384:768], 0.0, A.mult, A.add, reads=["rsC", "FL1"], writes=["FS"])
-    for s in range(N):
-        act(T.tokw[0:1, blk[s]], T.tokr[0:1, blk[s]], F.Identity, reads=["tokr"], writes=["tokw"], part=True, bias=float(s * TK))
-    v("tt", T.mp[:, :], T.mm[:, :], T.pc[:, :], A.add, reads=["mm", "pc"], writes=["mp"])
-    v("ts", T.gg[:, 0:1], T.rk[:, 0:1], float(DF), OUT, A.is_ge, A.mult, reads=["rk"], writes=["gg"], part=True)
-    v("ts", T.gg[:, 1:2], T.FS[:, 383:384], float(DF), OUT, A.is_ge, A.mult, reads=["FS"], writes=["gg"], part=True)
+        k, e8 = 8 * h, T.eb[:, h:h + 1]
+        act(T.mj[:, k:k + 7], T.Rm[:, k:k + 7], F.Sign, reads=["Rm%d" % h], writes=["mm%d" % h],
+            bias=T.Rm[:, k + 6:k + 7], scale=-1.0, accum_out=T.mm[:, h:h + 1])
+        act(T.SJ[:, row[h]], T.E1[:, :], F.Sign, reads=["E1", "eb%d" % h], writes=["sg%d" % h],
+            bias=e8, scale=-1.0, accum_out=T.sg[:, h:h + 1])
+        v("ts", T.EQ[:, row[h]], T.E1[:, :], e8, None, A.is_equal, reads=["E1", "eb%d" % h], writes=["EQ%d" % h])
+
+    def rank(h):
+        v("scan", T.FS[:, row[h]], T.sgn[:, row[h]], T.EQ[:, row[h]], T.sg[:, h:h + 1], A.mult, A.add,
+          reads=["sgn", "EQ%d" % h, "sg%d" % h], writes=["FS%d" % h])
+    rank(0)
     for h in range(2):
-        v("ts", T.fb2[:, blk[h]], T.zb[:, 0:32], T.gg[:, h:h + 1], T.mp[:, h:h + 1], A.add, A.add,
-          reads=["zb", "gg", "mp"], writes=["fb2"], part=True)
-    v("tr", T.ft2[:, :], T.fb2[:, :], reads=["fb2"], writes=["ft2"])
+        v("ts", T.mp[:, h:h + 1], T.mm[:, h:h + 1], 2.0, T.pc[:, h:h + 1], A.mult, A.add, reads=["mm%d" % h, "pc"], writes=["mp%d" % h])
+    rank(1)
     for h in range(2):
-        for a in range(4):
-            v("copy", T.fr2[0:32, blk[4 * h + a]], T.ft2[blk[a], blk[h]], reads=["ft2"], writes=["fr2"], part=True)
-    v("copy", T.fr2[32:64, :], T.fr2[0:32, :], reads=["fr2"], writes=["fr2a"])
-    v("copy", T.fr2[64:128, :], T.fr2[0:64, :], reads=["fr2", "fr2a"], writes=["fr2b"])
+        v("ts", T.fb2[:, blk[h]], T.c128[:, :], T.FS[:, SL * h + SL - 1:SL * h + SL], T.mp[:, h:h + 1], A.is_ge, A.add,
+          reads=["c128", "FS%d" % h, "mp%d" % h], writes=["fb2"], part=True)
+    v("tr", T.ft2[:, :, :], T.fb2[:, :], reads=["fb2"], writes=["ft2"])
+    for a in range(4):
+        v("copy", T.fr2[0:32, :, blk[a]], T.ft2[blk[a], :, :], reads=["ft2"], writes=["fr2"], part=True)
+    for b in range(1, 4):
+        v("copy", T.fr2[blk[b], :, :], T.fr2[0:32, :, :], reads=["fr2"], writes=["fr2a"], part=True)
     for u in range(2):
-        v("ts", T.M2[:, 256 * u:256 * u + 256], T.fr2[:, :], T.mcol[:, u:u + 1], None, A.is_equal,
-          reads=["fr2", "fr2a", "fr2b", "mcol"], writes=["M2"], part=True)
-    v("scan", T.C2[:, :], T.rsB[:, :], T.M2[:, :], 0.0, A.mult, A.add, reads=["rsB", "M2"], writes=["C2"])
+        v("ts", T.M2[:, row[u]], T.fr2[:, :, :], T.mcol[:, u:u + 1], None, A.is_equal,
+          reads=["fr2", "fr2a", "mcol"], writes=["M2"], part=True)
+    v("scan", T.C2[:, :], T.one[:, :], T.M2[:, :], 0.0, A.mult, A.add, reads=["one", "M2"], writes=["C2"])
     v("ts", T.L2[:, :], T.C2[:, :], T.thr1[:, 0:1], None, A.is_le, reads=["C2", "thr1"], writes=["L2"])
-    v("scan", T.S2[:, :], T.rsB[:, :], T.L2[:, :], 0.0, A.mult, A.add, reads=["rsB", "L2"], writes=["S2"])
+    v("scan", T.S2[:, :], T.one[:, :], T.L2[:, :], 0.0, A.mult, A.add, reads=["one", "L2"], writes=["S2"])
     for b in range(4):
-        v("ts", T.off2[0:32, 4 * b:4 * b + 4:2], T.S2[blk[b], 255:512:256], 0.0, None, A.add, reads=["S2"], writes=["off2"], part=True)
-    v("ts", T.off2[0:32, 1:16:2], T.off2[0:32, 0:16:2], float(HO), None, A.add, reads=["off2"], writes=["off2h"])
-    v("copy", T.off2[32:64, :], T.off2[0:32, :], reads=["off2", "off2h"], writes=["off2a"])
-    v("copy", T.off2[64:128, :], T.off2[0:64, :], reads=["off2", "off2h", "off2a"], writes=["off2b"])
-    O2 = ["off2", "off2h", "off2a", "off2b"]
+        v("ts", T.off2[0:32, 4 * b:4 * b + 4:2], T.S2[blk[b], SL - 1:2 * SL:SL], 0.0, None, A.add, reads=["S2"], writes=["off2"], part=True)
+    for b in range(4):
+        if b:
+            v("ts", T.off2[blk[b], 0:16:2], T.off2[0:32, 0:16:2], 0.0, None, A.add, reads=["off2"], writes=["off2a"], part=True)
+        v("ts", T.off2[blk[b], 1:16:2], T.off2[0:32, 0:16:2], float(HO), None, A.add, reads=["off2"], writes=["off2a"], part=True)
+    O2 = ["off2", "off2a"]
     XR = O2 + ["xh", "xhz", "h0", "h1"]
     v("copy", T.s2q[:, :].bitcast(u32), T.xh[:, 0:XW].bitcast(u32).indirect(T.off2[:, :]), reads=XR, writes=["s2q"])
     act(T.s2s[:, :], T.xhs[:, 0:XW].indirect(T.off2[:, :]), F.Copy, reads=XR, writes=["s2s"])
     send(others, 0, "a2", lambda d: T.s2q[:, blk[d]].bitcast(u8), lambda d: T.l2q[:, blk[me]].bitcast(u8), ["s2q"])
     send(others, 1, "a2", lambda d: T.s2s[:, blk[d]], lambda d: T.l2s[:, blk[me]], ["s2s"])
 
-    act(T.wr[:, :], T.tokw[:, :].indirect(T.off2[:, :]), F.Copy, reads=O2 + ["tokw"], writes=["wr"])
+    v("tt", T.tokw[0:1, 0:SL], T.tokr[0:1, :], T.soff[0:1, :], A.add, reads=["tokr", "soff", "tokm"], writes=["tokw"])
+    v("copy", T.wr[:, :], T.tokw[:, 0:XW].indirect(T.off2[:, :]), reads=O2 + ["tokw", "tokm"], writes=["wr"])
     dma("s", "wd", T.whod[:, 0:2 * CB, 0], T.wr[0:1, :], reads=["wr"], writes=["whod"])
     send(others, 0, "aw", lambda d: T.whod[d], lambda d: T.whol[me], ["whod"])
     v("qz", T.vxq[:, :], T.vxs[:, :], T.vxt[:, :], reads=["vxt"], writes=["vxq"])
     v("qz", T.vhq[:, :], T.vhs[:, :], T.vht[:, :], reads=["vht"], writes=["vhq"])
 
     lands("l2", "a2", 0, 1)
-    Y = [T.p0, T.p5]
+    Y, yt = [T.p0, T.p5], ["p0", "p5"]
     for q in range(2):
-        k, j, t = slice(112 * q, 112 * q + 128), slice(112 * q + CB, 112 * q + CB + 128), ["p0", "p5"][q]
+        k, j, t = slice(112 * q, 112 * q + 128), slice(112 * q + CB, 112 * q + CB + 128), yt[q]
         mm(Y[q][:, 0:128], T.vxq[:, :], T.vxs[:, :], T.l2q[:, k], T.l2s[:, k], True, False, reads=["vxq", "l2"], writes=[t])
         mm(Y[q][:, 0:128], T.vhq[:, :], T.vhs[:, :], T.l2q[:, j], T.l2s[:, j], False, True, reads=["vhq", "l2"], writes=[t], part=True)
     v("copy", T.hq[:, :].bitcast(u32), T.l2q[:, :].bitcast(u32).indirect(T.offh[:, :]), reads=["l2", "offh"], writes=["hq"])
     act(T.hs[:, :], T.l2s[:, :].indirect(T.offh[:, :]), F.Copy, reads=["l2", "offh"], writes=["hs"])
     for a in range(N):
         k = 32 * a - 112 * (a // 4)
-        v("copy", T.ysb[:, CB * a:CB * a + CB], Y[a // 4][:, k:k + CB], reads=[["p0", "p5"][a // 4]], writes=["ysb"], part=True)
+        o, i = T.ysb[:, CB * a:CB * a + CB], Y[a // 4][:, k:k + CB]
+        if a < 4:
+            v("copy", o, i, reads=[yt[0]], writes=["ysb"], part=True)
+        else:
+            act(o, i, F.Copy, reads=[yt[1]], writes=["ysb"], part=True)
     dma("s", "oc", T.oc[:, :], T.hq[:, :].bitcast(u8), reads=["hq"], writes=["oc"])
+    dma("s", "y", T.y[:, :], T.ysb[:, :], reads=["ysb"], writes=["y"])
     for k in range(4):
         dma("a", "o%d" % k, T.osc[4 * k:4 * k + 4, :], T.hs[32 * k:32 * k + 4, :], reads=["hs"], writes=["osc%d" % k])
-    dma("s", "y", T.y[:, :], T.ysb[:, :], reads=["ysb"], writes=["y"])
     lands("whol", "aw", 0)
     dma("s", "who", T.who[0:1, :], T.whol[:, 0:CB, 0], reads=["whol"], writes=["who"])
     for sem in sorted(cnt):

@@ -9,8 +9,7 @@ DF = 64
 SL = N * CAPP
 HO = 384
 XW = 642
-BIG = 1e29
-OUT = 200.0
+BIG = 2.0 ** 96
 
 SCRATCH = {}
 
@@ -26,13 +25,13 @@ _declare("sbuf", "uint8", xs=136, rs=128, ws=512, r2s=128, r8s=128, vxs=128, vhs
 _declare("dram", "bfloat16", fd=[128, 1], fl=[N, 128, 1], tokd=[N, 128, 1], tokl=[N, 128, 1])
 _declare("dram", "float32", whod=[N, 128, 1], whol=[N, 128, 1])
 _declare("sbuf", "int32", pp=8, cc=8, ig=8, ih=8, p15=8, p31=8, pb=8)
-_declare("sbuf", "float32", thr1=2, ccol=1, ecol=2, mgt=2, mct=2, mcol=2, neg8=8, io32=32, m1=128)
-_declare("sbuf", "bfloat16", zb=128, rsA=512, c128=32, one=2 * SL, sgn=2 * SL, soff=SL, tokv=144)
+_declare("sbuf", "float32", thr1=2, thrh=2, ccol=1, ecol=2, mgt=2, mct=2, mcol=2, neg8=8, lim8=8, io32=32, m1=128)
+_declare("sbuf", "bfloat16", zb=128, rsA=512, c128=32, one=2 * SL, sgn=2 * SL, tokv=144)
 _declare("sbuf", "uint16", offz=2, offh=8, off1=16, off2=16)
-_declare("sbuf", "float32", R=8, lt=8, first=1, nb=[32, 1], nbb=[32, 32], nrep=32, pc=2, pen=SL,
-         E1=SL, eb=2, Rm=16, mj=16, mm=2, sg=2, tokw=648, wr=SL, ysb=128)
-_declare("sbuf", "bfloat16", fb=32, fr=128, M1=256, C1=256, L1=512, S1=512, trow=SL, tokr=SL, frl=[32, 128], feq=[32, 128],
-         EQ=2 * SL, FS=2 * SL, SJ=2 * SL, mp=2, fb2=64, ft2=[128, 2, 32], fr2=[128, 2, 128], M2=2 * SL, C2=2 * SL, L2=2 * SL, S2=2 * SL)
+_declare("sbuf", "float32", R=8, first=1, sa=4, lf1=[32, 16], lf2=[32, 8], nb=[32, 1], nbb=[32, 32], nrep=32, nrepb=8, pen=SL,
+         E1=SL, Rm=18, mj=16, mm=2, sg=2, tokw=648, wr=SL, ysb=128)
+_declare("sbuf", "bfloat16", fb=32, fr=128, M1=256, C1=256, L1=512, S1=256, trow=SL, tokr=SL, frl=[32, 128], feq=[32, 128],
+         EQ=2 * SL, FS=2 * SL, SJ=2 * SL, mp=2, fb2=64, fr2=[128, 4, 64], M2=2 * SL, C2=2 * SL, L2=SL, S2=SL)
 _declare("psum", "float32", p0=512, p1=512, p2=512, p3=512, p4=512, p5=512, p6=512, p7=512)
 _DMAS = ["x", "rt", "w", "r2a", "r2b", "vx", "vh", "fd", "fo", "fl", "td", "to", "tl", "wd", "wo", "ti", "wi",
          "y", "oc", "o0", "o1", "o2", "o3", "who"]
@@ -165,6 +164,7 @@ def rank_program(g, core, T, topo):
     for k in range(4):
         act(T.rsA[:, half[k]], T.zb[:, :], F.Identity, reads=["zb"], writes=["rsA1"], part=True, bias=1.0)
     act(T.rsA[:, 0:512:128], T.zb[:, 0:4], F.Copy, reads=["zb", "rsA1"], writes=["rsA"])
+    act(T.thrh[:, :], T.thr1[:, :], F.Identity, reads=["thr1"], writes=["thrh"], bias=0.5)
     dma("a", "wo", T.whol[me:me + 1, 0:CB, 0], T.m1[0:1, 0:CB], reads=["m1"], writes=["whol"], part=True)
     dma("a", "wi", T.whod[:, :, 0], T.m1[0:N, :], reads=["m1"], writes=["whod"])
     dma("a", "ti", T.tokd[:, :, 0], T.zb[0:N, :], reads=["zb"], writes=["tokd"])
@@ -173,31 +173,33 @@ def rank_program(g, core, T, topo):
     v("qz", T.xq[:, 0:130], T.xs[:, 0:130], T.xt[:, :], reads=["xt"], writes=["xq"])
     mm(T.p0[:, 0:128], T.xq[:, 0:128], T.xs[:, 0:128], T.rq[:, :], T.rs[:, :], True, True, reads=["xq", "rq"], writes=["p0"])
     v("scan", T.R[:, :], T.p0[:, 0:8], T.neg8[:, :], -9e29, A.max, A.max, reads=["p0", "neg8"], writes=["R"])
-    v("ts", T.lt[:, :], T.R[:, :], T.R[:, 7:8], None, A.is_lt, reads=["R"], writes=["lt"])
-    red(v, T.first[:, :], T.lt[:, :], reads=["lt"], writes=["first"])
+    act(T.mj[:, 0:8], T.R[:, :], F.Sign, reads=["R"], writes=["first"], bias=T.R[:, 7:8], scale=-1.0, accum_out=T.first[:, 0:1])
     v("ts", T.fb[:, :], T.zb[:, 0:32], T.first[:, 0:1], None, A.add, reads=["zb", "first"], writes=["fb"])
     dma("s", "fd", T.fd[:, :], T.fb[:, 0:1], reads=["fb"], writes=["fd"])
     dma("s", "fo", T.fl[me], T.fb[:, 0:1], reads=["fb"], writes=["fl"], part=True)
     send(near, 2, "af", lambda d: T.fb[:, 0:1], lambda d: T.fl[me], ["fb"])
-    v("tr", T.fr[:, 0:32], T.fb[:, :], reads=["fb"], writes=["frT"])
-    for a in range(1, 4):
-        v("copy", T.fr[0:32, blk[a]], T.fr[blk[a], 0:32], reads=["frT"], writes=["fr"], part=True)
-    for b in range(1, 4):
-        v("copy", T.fr[blk[b], :], T.fr[0:32, :], reads=["fr", "frT"], writes=["fra"], part=b > 1)
+    for a in range(4):
+        v("tr", T.fr[0:32, blk[a]], T.fb[blk[a], :], reads=["fb"], writes=["fr"], part=True)
+    act(T.fr[blk[3], :], T.fr[0:32, :], F.Copy, reads=["fr"], writes=["frc"])
+    for b in range(1, 3):
+        v("copy", T.fr[blk[b], :], T.fr[0:32, :], reads=["fr"], writes=["fra"], part=b > 1)
     for u in range(2):
         v("ts", T.M1[:, half[u]], T.fr[:, :], T.ecol[:, u:u + 1], None, A.is_equal,
-          reads=["fr", "fra", "ecol"], writes=["M1"], part=True)
-    v("scan", T.C1[:, :], T.rsA[:, 0:256], T.M1[:, :], 0.0, A.mult, A.add, reads=["rsA", "M1"], writes=["C1"])
+          reads=["fr", "fra", "frc", "ecol"], writes=["M1%d" % u])
     for u in range(2):
-        for h in range(2):
-            v("ts", T.L1[:, half[2 * u + h]], T.C1[:, half[u]], T.thr1[:, h:h + 1], None, A.is_le,
-              reads=["C1", "thr1"], writes=["L1"], part=True)
-    v("scan", T.S1[:, :], T.rsA[:, :], T.L1[:, :], 0.0, A.mult, A.add, reads=["rsA", "L1"], writes=["S1"])
+        v("scan", T.C1[:, half[u]], T.rsA[:, half[u]], T.M1[:, half[u]], 0.0, A.mult, A.add, reads=["rsA", "M1%d" % u], writes=["C1%d" % u])
+    for h in range(2):
+        act(T.L1[:, half[2 + h]], T.C1[:, half[0]], F.Sign, reads=["C10", "thrh"], writes=["sa"], part=True,
+            bias=T.thrh[:, h:h + 1], scale=-1.0, accum_out=T.sa[:, h:h + 1])
+        v("ts", T.L1[:, half[h]], T.C1[:, half[1]], T.thr1[:, h:h + 1], None, A.is_le, reads=["C11", "thr1"], writes=["L1%d" % h])
+    for h in range(2):
+        v("scan", T.S1[:, half[h]], T.rsA[:, half[h]], T.L1[:, half[h]], 0.0, A.mult, A.add, reads=["rsA", "L1%d" % h], writes=["S1"], part=True)
     for b in range(4):
-        v("ts", T.off1[0:32, 4 * b:4 * b + 4], T.S1[blk[b], 127:512:128], 0.0, None, A.add, reads=["S1"], writes=["off1"], part=True)
-    for b in range(1, 4):
-        v("copy", T.off1[blk[b], :], T.off1[0:32, :], reads=["off1"], writes=["off1a"], part=True)
-    O1 = ["off1", "off1a", "xq"]
+        act(T.lf1[0:32, 4 * b:4 * b + 2], T.sa[blk[b], 0:2], F.Identity, reads=["sa"], writes=["lf1"], part=True, bias=64.0, scale=0.5)
+        v("copy", T.lf1[0:32, 4 * b + 2:4 * b + 4], T.S1[blk[b], 127:256:128], reads=["S1"], writes=["lf1"], part=True)
+    for b in range(4):
+        v("copy", T.off1[blk[b], :], T.lf1[0:32, :], reads=["lf1"], writes=["off1"], part=True)
+    O1 = ["off1", "xq"]
     ms = slice(2 * me, 2 * me + 2)
     v("copy", T.sq[:, :].bitcast(u32), T.xq[:, 0:130].bitcast(u32).indirect(T.off1[:, :]), reads=O1, writes=["sq"])
     act(T.ss[:, :], T.xs[:, 0:130].indirect(T.off1[:, :]), F.Copy, reads=O1, writes=["ss"])
@@ -237,13 +239,14 @@ def rank_program(g, core, T, topo):
     v("tt", T.ih[:, :], T.ig[:, :], T.p15[:, :], A.add, reads=["ig", "p15"], writes=["ih"])
     v("tt", T.mct[:, :], T.ecol[:, :], T.mgt[:, :], A.add, reads=["ecol", "mgt"], writes=["mct"])
     v("copy", T.offh[:, :], T.ih[:, :], reads=["ih"], writes=["offh"])
-    v("ts", T.mcol[:, :], T.mct[:, :], 2.0, None, A.mult, reads=["mct"], writes=["mcol"])
+    v("ts", T.mcol[:, :], T.mct[:, :], 1.0, None, A.add, reads=["mct"], writes=["mcol"])
+    v("set", T.lim8[:, 0:7], 9e29, writes=["lim8"], part=True)
+    v("set", T.lim8[:, 7:8], -9e29, writes=["lim8"], part=True)
     v("set", T.c128[:, :], 128.0, writes=["c128"])
     v("set", T.one[:, 0:2 * SL:SL], 0.0, reads=["one1"], writes=["one"])
     for h in range(2):
         k = slice(SL * h + 128 * h, SL * h + 128 * h + 128)
         gp("sel", T.sgn[:, k], T.sgn[:, k], [[-1, 128]], A.not_equal, -1.0, 0, 1, reads=["sgn1"], writes=["sgn"], part=True)
-    gp("iota", T.soff[:, :], [[TK, N], [0, CAPP]], 0, 0, writes=["soff"], **fl)
     send(others, 0, "at", lambda d: T.tokd[d], lambda d: T.tokl[me], ["tokd"])
 
     v("ts", T.feq[0:8, :], T.frl[0:8, :], float(me), None, A.is_equal, reads=["frl"], writes=["feq"])
@@ -259,12 +262,20 @@ def rank_program(g, core, T, topo):
             v("ts", T.pen[:, blk[s]], T.io32[:, :], T.nrep[:, s:s + 1], BIG, A.is_ge, A.mult,
               reads=NR + ["io32"], writes=["pen%d" % (s // 4)], part=True)
 
+    def nbs():
+        act(T.nrepb[:, :], T.nrep[:, 0:8], F.Identity, reads=NR, writes=["nrepb"], bias=BIG, scale=-BIG)
+
+    def pns(*ranks):
+        for s in ranks:
+            act(T.pen[:, blk[s]], T.io32[:, :], F.Relu, reads=["nrepb", "io32"], writes=["pen%d" % (s // 4)], part=True,
+                bias=T.nrepb[:, s:s + 1], scale=BIG)
+
     def pcs(*blocks):
         for a in blocks:
-            v("ts", T.pc[blk[a], :], T.nrep[blk[a], a:8:4], T.ccol[blk[a], 0:1], OUT, A.is_le, A.mult,
-              reads=NR + ["ccol"], writes=["pc"], part=True)
-    fill = {(0, 1): [(pens, 0, 1)], (0, 3): [(pens, 2, 3)], (0, 4): [(pens, 4, 5)],
-            (1, 1): [(pens, 6, 7)], (1, 3): [(pcs, 0, 1)], (1, 4): [(pcs, 2, 3)]}
+            v("ts", T.Rm[blk[a], 0:18:9], T.nrep[blk[a], a:8:4], T.ccol[blk[a], 0:1], -9e29, A.is_gt, A.mult,
+              reads=NR + ["ccol"], writes=["Rmc"], part=True)
+    fill = {(0, 0): [(nbs,), (pns, 4)], (0, 2): [(pns, 5)], (1, 0): [(pns, 6, 7)],
+            (0, 1): [(pens, 0, 1)], (0, 3): [(pens, 2)], (1, 1): [(pens, 3), (pcs, 0)], (1, 3): [(pcs, 1)], (1, 4): [(pcs, 2, 3)]}
     lands("tokl", "at", 0)
     dma("s", "tl", T.tokr[0:1, :], T.tokl[:, 0:CAPP, 0], reads=["tokl"], writes=["tokr"])
     dma("s", "vx", T.vxt[:, :], T.vx[:, :], writes=["vxt"])
@@ -289,10 +300,10 @@ def rank_program(g, core, T, topo):
             o = T.ht[:, 512 * h + i:e:4]
             if i % 2:
                 v("ts", o, P[h][i][:, 0:128], 0.0, 0.0625, A.max, A.mult, reads=[B[h][i]], writes=["ht%d" % h], part=True)
-                for f, *n in fill.get((h, i), []):
-                    f(*n)
             else:
                 act(o, P[h][i][:, 0:128], F.Relu, reads=[B[h][i]], writes=["ht%d" % h], part=True, scale=0.0625)
+            for f, *n in fill.get((h, i), []):
+                f(*n)
         k = slice(HO + 128 * h, XW if h else HO + 128)
         v("qz", T.xh[:, k], T.xhs[:, k], T.ht[:, 512 * h:e + 8 * h], reads=["ht%d" % h, "htz"], writes=["h%d" % h])
         products(h)
@@ -300,9 +311,8 @@ def rank_program(g, core, T, topo):
             f(*n)
 
     def second(h):
-        k = 8 * h
-        v("copy", T.eb[:, h:h + 1], PE[h][:, 7:8], reads=[pe[h]], writes=["eb%d" % h])
-        v("scan", T.Rm[:, k:k + 7], PE[h][:, 0:7], T.neg8[:, 0:7], -9e29, A.max, A.max, reads=[pe[h], "neg8"], writes=["Rm%d" % h])
+        k = 9 * h
+        v("scan", T.Rm[:, k + 1:k + 9], T.lim8[:, :], PE[h][:, 0:8], -9e29, A.min, A.max, reads=[pe[h], "lim8"], writes=["Rm%d" % h])
 
     def away(h):
         v("tt", T.E1[:, half[h]], ROW[h][:, 0:128], T.pen[:, half[h]], A.add, reads=[rw[h], "pen%d" % h], writes=["E1"], part=True)
@@ -310,50 +320,63 @@ def rank_program(g, core, T, topo):
     away(0)
     away(1)
     second(1)
+
+    def number(h):
+        k = 9 * h
+        act(T.mj[:, 8 * h:8 * h + 8], T.Rm[:, k:k + 8], F.Sign, reads=["Rm%d" % h, "Rmc"], writes=["mm%d" % h],
+            bias=T.Rm[:, k + 7:k + 8], scale=-1.0, accum_out=T.mm[:, h:h + 1])
+        act(T.mp[:, h:h + 1], T.mm[:, h:h + 1], F.Copy, reads=["mm%d" % h], writes=["mp%d" % h])
+    number(0)
     for h in range(2):
-        k, e8 = 8 * h, T.eb[:, h:h + 1]
-        act(T.mj[:, k:k + 7], T.Rm[:, k:k + 7], F.Sign, reads=["Rm%d" % h], writes=["mm%d" % h],
-            bias=T.Rm[:, k + 6:k + 7], scale=-1.0, accum_out=T.mm[:, h:h + 1])
-        act(T.SJ[:, row[h]], T.E1[:, :], F.Sign, reads=["E1", "eb%d" % h], writes=["sg%d" % h],
+        e8 = T.Rm[:, 9 * h + 8:9 * h + 9]
+        act(T.SJ[:, row[h]], T.E1[:, :], F.Sign, reads=["E1", "Rm%d" % h], writes=["sg%d" % h],
             bias=e8, scale=-1.0, accum_out=T.sg[:, h:h + 1])
-        v("ts", T.EQ[:, row[h]], T.E1[:, :], e8, None, A.is_equal, reads=["E1", "eb%d" % h], writes=["EQ%d" % h])
+        v("ts", T.EQ[:, row[h]], T.E1[:, :], e8, None, A.is_equal, reads=["E1", "Rm%d" % h], writes=["EQ%d" % h])
+    number(1)
 
     def rank(h):
         v("scan", T.FS[:, row[h]], T.sgn[:, row[h]], T.EQ[:, row[h]], T.sg[:, h:h + 1], A.mult, A.add,
           reads=["sgn", "EQ%d" % h, "sg%d" % h], writes=["FS%d" % h])
     rank(0)
-    for h in range(2):
-        v("ts", T.mp[:, h:h + 1], T.mm[:, h:h + 1], 2.0, T.pc[:, h:h + 1], A.mult, A.add, reads=["mm%d" % h, "pc"], writes=["mp%d" % h])
     rank(1)
     for h in range(2):
-        v("ts", T.fb2[:, blk[h]], T.c128[:, :], T.FS[:, SL * h + SL - 1:SL * h + SL], T.mp[:, h:h + 1], A.is_ge, A.add,
+        v("ts", T.fb2[:, blk[h]], T.c128[:, :], T.FS[:, SL * h + SL - 1:SL * h + SL], T.mp[:, h:h + 1], A.is_lt, A.mult,
           reads=["c128", "FS%d" % h, "mp%d" % h], writes=["fb2"], part=True)
-    v("tr", T.ft2[:, :, :], T.fb2[:, :], reads=["fb2"], writes=["ft2"])
     for a in range(4):
-        v("copy", T.fr2[0:32, :, blk[a]], T.ft2[blk[a], :, :], reads=["ft2"], writes=["fr2"], part=True)
-    for b in range(1, 4):
-        v("copy", T.fr2[blk[b], :, :], T.fr2[0:32, :, :], reads=["fr2"], writes=["fr2a"], part=True)
+        v("tr", T.fr2[0:32, a, :], T.fb2[blk[a], :], reads=["fb2"], writes=["fr2"], part=True)
+    act(T.fr2[blk[3], :, :], T.fr2[0:32, :, :], F.Copy, reads=["fr2"], writes=["fr2c"])
+    for b in range(1, 3):
+        v("copy", T.fr2[blk[b], :, :], T.fr2[0:32, :, :], reads=["fr2"], writes=["fr2a"], part=b > 1)
     for u in range(2):
-        v("ts", T.M2[:, row[u]], T.fr2[:, :, :], T.mcol[:, u:u + 1], None, A.is_equal,
-          reads=["fr2", "fr2a", "mcol"], writes=["M2"], part=True)
-    v("scan", T.C2[:, :], T.one[:, :], T.M2[:, :], 0.0, A.mult, A.add, reads=["one", "M2"], writes=["C2"])
-    v("ts", T.L2[:, :], T.C2[:, :], T.thr1[:, 0:1], None, A.is_le, reads=["C2", "thr1"], writes=["L2"])
-    v("scan", T.S2[:, :], T.one[:, :], T.L2[:, :], 0.0, A.mult, A.add, reads=["one", "L2"], writes=["S2"])
+        for h in range(2):
+            v("ts", T.M2[:, half[2 * u + h]], T.fr2[:, :, blk[h]], T.mcol[:, u:u + 1], None, A.is_equal,
+              reads=["fr2", "fr2a", "fr2c", "mcol"], writes=["M2%d" % u], part=True)
+    for u in range(2):
+        v("scan", T.C2[:, row[u]], T.one[:, row[u]], T.M2[:, row[u]], 0.0, A.mult, A.add, reads=["one", "M2%d" % u], writes=["C2%d" % u])
+    act(T.SJ[:, row[0]], T.C2[:, row[0]], F.Sign, reads=["C20", "thrh"], writes=["sa2"],
+        bias=T.thrh[:, 0:1], scale=-1.0, accum_out=T.sa[:, 2:3])
+    for h in range(2):
+        v("ts", T.L2[:, half[h]], T.C2[:, half[2 + h]], T.thr1[:, 0:1], None, A.is_le, reads=["C21", "thr1"], writes=["L2%d" % h])
+    for h in range(2):
+        v("scan", T.S2[:, half[h]], T.one[:, half[h]], T.L2[:, half[h]], 0.0, A.mult, A.add, reads=["one", "L2%d" % h], writes=["S2"], part=True)
     for b in range(4):
-        v("ts", T.off2[0:32, 4 * b:4 * b + 4:2], T.S2[blk[b], SL - 1:2 * SL:SL], 0.0, None, A.add, reads=["S2"], writes=["off2"], part=True)
+        act(T.lf2[0:32, 2 * b:2 * b + 1], T.sa[blk[b], 2:3], F.Identity, reads=["sa2"], writes=["lf2"], part=True, bias=128.0, scale=0.5)
+        v("tt", T.lf2[0:32, 2 * b + 1:2 * b + 2], T.S2[blk[b], 127:128], T.S2[blk[b], 255:256], A.add, reads=["S2"], writes=["lf2"], part=True)
+    for s in range(N):
+        act(T.tokw[0:1, blk[s]], T.tokr[0:1, blk[s]], F.Identity, reads=["tokr", "tokm"], writes=["tokw"], part=True, bias=float(TK * s))
     for b in range(4):
-        if b:
-            v("ts", T.off2[blk[b], 0:16:2], T.off2[0:32, 0:16:2], 0.0, None, A.add, reads=["off2"], writes=["off2a"], part=True)
-        v("ts", T.off2[blk[b], 1:16:2], T.off2[0:32, 0:16:2], float(HO), None, A.add, reads=["off2"], writes=["off2a"], part=True)
-    O2 = ["off2", "off2a"]
+        v("copy", T.off2[blk[b], 0:16:2], T.lf2[0:32, :], reads=["lf2"], writes=["off2%d" % (b // 2)], part=True)
+    for k in range(2):
+        q = slice(64 * k, 64 * k + 64)
+        v("ts", T.off2[q, 1:16:2], T.off2[q, 0:16:2], float(HO), None, A.add, reads=["off2%d" % k], writes=["off2a"], part=True)
+    O2 = ["off20", "off21", "off2a"]
     XR = O2 + ["xh", "xhz", "h0", "h1"]
     v("copy", T.s2q[:, :].bitcast(u32), T.xh[:, 0:XW].bitcast(u32).indirect(T.off2[:, :]), reads=XR, writes=["s2q"])
+    act(T.wr[:, :], T.tokw[:, 0:XW].indirect(T.off2[:, :]), F.Copy, reads=O2 + ["tokw", "tokm"], writes=["wr"])
     act(T.s2s[:, :], T.xhs[:, 0:XW].indirect(T.off2[:, :]), F.Copy, reads=XR, writes=["s2s"])
     send(others, 0, "a2", lambda d: T.s2q[:, blk[d]].bitcast(u8), lambda d: T.l2q[:, blk[me]].bitcast(u8), ["s2q"])
     send(others, 1, "a2", lambda d: T.s2s[:, blk[d]], lambda d: T.l2s[:, blk[me]], ["s2s"])
 
-    v("tt", T.tokw[0:1, 0:SL], T.tokr[0:1, :], T.soff[0:1, :], A.add, reads=["tokr", "soff", "tokm"], writes=["tokw"])
-    v("copy", T.wr[:, :], T.tokw[:, 0:XW].indirect(T.off2[:, :]), reads=O2 + ["tokw", "tokm"], writes=["wr"])
     dma("s", "wd", T.whod[:, 0:2 * CB, 0], T.wr[0:1, :], reads=["wr"], writes=["whod"])
     send(others, 0, "aw", lambda d: T.whod[d], lambda d: T.whol[me], ["whod"])
     v("qz", T.vxq[:, :], T.vxs[:, :], T.vxt[:, :], reads=["vxt"], writes=["vxq"])
@@ -362,27 +385,28 @@ def rank_program(g, core, T, topo):
     lands("l2", "a2", 0, 1)
     Y, yt = [T.p0, T.p5], ["p0", "p5"]
     for q in range(2):
-        k, j, t = slice(112 * q, 112 * q + 128), slice(112 * q + CB, 112 * q + CB + 128), yt[q]
-        mm(Y[q][:, 0:128], T.vxq[:, :], T.vxs[:, :], T.l2q[:, k], T.l2s[:, k], True, False, reads=["vxq", "l2"], writes=[t])
-        mm(Y[q][:, 0:128], T.vhq[:, :], T.vhs[:, :], T.l2q[:, j], T.l2s[:, j], False, True, reads=["vhq", "l2"], writes=[t], part=True)
+        n, t = (144, 128)[q], yt[q]
+        k, j = slice(112 * q, 112 * q + n), slice(112 * q + CB, 112 * q + CB + n)
+        mm(Y[q][:, 0:n], T.vxq[:, :], T.vxs[:, :], T.l2q[:, k], T.l2s[:, k], True, False, reads=["vxq", "l2"], writes=[t])
+        mm(Y[q][:, 0:n], T.vhq[:, :], T.vhs[:, :], T.l2q[:, j], T.l2s[:, j], False, True, reads=["vhq", "l2"], writes=[t], part=True)
     v("copy", T.hq[:, :].bitcast(u32), T.l2q[:, :].bitcast(u32).indirect(T.offh[:, :]), reads=["l2", "offh"], writes=["hq"])
     act(T.hs[:, :], T.l2s[:, :].indirect(T.offh[:, :]), F.Copy, reads=["l2", "offh"], writes=["hs"])
     for a in range(N):
-        k = 32 * a - 112 * (a // 4)
-        o, i = T.ysb[:, CB * a:CB * a + CB], Y[a // 4][:, k:k + CB]
-        if a < 4:
+        k = 32 * a - 112 * (a // 5)
+        o, i = T.ysb[:, CB * a:CB * a + CB], Y[a // 5][:, k:k + CB]
+        if a < 5:
             v("copy", o, i, reads=[yt[0]], writes=["ysb"], part=True)
         else:
             act(o, i, F.Copy, reads=[yt[1]], writes=["ysb"], part=True)
     dma("s", "oc", T.oc[:, :], T.hq[:, :].bitcast(u8), reads=["hq"], writes=["oc"])
-    dma("s", "y", T.y[:, :], T.ysb[:, :], reads=["ysb"], writes=["y"])
     for k in range(4):
-        dma("a", "o%d" % k, T.osc[4 * k:4 * k + 4, :], T.hs[32 * k:32 * k + 4, :], reads=["hs"], writes=["osc%d" % k])
+        dma("s" if k < 2 else "a", "o%d" % k, T.osc[4 * k:4 * k + 4, :], T.hs[32 * k:32 * k + 4, :], reads=["hs"], writes=["osc%d" % k])
+    dma("s", "y", T.y[:, :], T.ysb[:, :], reads=["ysb"], writes=["y"])
     lands("whol", "aw", 0)
     dma("s", "who", T.who[0:1, :], T.whol[:, 0:CB, 0], reads=["whol"], writes=["who"])
     for sem in sorted(cnt):
         if max(seen[q].get(sem, 0) for q in eng) < cnt[sem]:
-            need("a" if sem[:3] == "d_o" and sem != "d_oc" else "s" if sem[:2] == "d_" else "g", [(sem, cnt[sem])])
+            need("a" if sem in ("d_o2", "d_o3") else "s" if sem[:2] == "d_" else "g", [(sem, cnt[sem])])
 
 
 def red(v, out, in_, **kw):

from concourse.bass import DstId, RemoteDMATransfer
from concourse.mybir import dt, AluOpType as A, AxisListType, ActivationFunctionType as F

N = 8
TK = 128
CAPP = 32
CB = 16
DF = 64
SL = N * CAPP
HO = 384
XW = 642
BIG = 2.0 ** 96

SCRATCH = {}


def _declare(kind, dtype, **bufs):
    for name, n in bufs.items():
        SCRATCH[name] = (kind, n if isinstance(n, list) else [128, n], dtype)


_declare("sbuf", "bfloat16", xt=520, rtt=512, wt=2048, r2t=512, r8t=512, vxt=512, vht=512, zt=512, ht=1032)
_declare("sbuf", "float8_e4m3fn_x4", xq=136, rq=128, wq=512, r2q=128, r8q=128, vxq=128, vhq=128, sq=SL, xh=648, s2q=SL, l2q=SL, hq=128)
_declare("sbuf", "uint8", xs=136, rs=128, ws=512, r2s=128, r8s=128, vxs=128, vhs=128, ss=SL, xhs=648, s2s=SL, l2s=SL, hs=128)
_declare("dram", "bfloat16", fd=[128, 1], fl=[N, 128, 1], tokd=[N, 128, 1], tokl=[N, 128, 1])
_declare("dram", "float32", whod=[N, 128, 1], whol=[N, 128, 1])
_declare("sbuf", "int32", pp=8, cc=8, ig=8, ih=8, p15=8, p31=8, pb=8)
_declare("sbuf", "float32", thr1=2, thrh=2, ccol=1, ecol=2, mgt=2, mct=2, mcol=2, neg8=8, lim8=8, io32=32, m1=128)
_declare("sbuf", "bfloat16", zb=128, rsA=512, c128=32, one=2 * SL, sgn=2 * SL, tokv=144)
_declare("sbuf", "uint16", offz=2, offh=8, off1=16, off2=16)
_declare("sbuf", "float32", R=8, first=1, sa=4, lf1=[32, 16], lf2=[32, 8], nb=[32, 1], nbb=[32, 32], nrep=32, nrepb=8, pen=SL,
         E1=SL, Rm=18, mj=16, mm=2, sg=2, tokw=648, wr=SL, ysb=128)
_declare("sbuf", "bfloat16", fb=32, fr=128, M1=256, C1=256, L1=512, S1=256, trow=SL, tokr=SL, frl=[32, 128], feq=[32, 128],
         EQ=2 * SL, FS=2 * SL, SJ=2 * SL, mp=2, fb2=64, fr2=[128, 4, 64], M2=2 * SL, C2=2 * SL, L2=SL, S2=SL)
_declare("psum", "float32", p0=512, p1=512, p2=512, p3=512, p4=512, p5=512, p6=512, p7=512)
_DMAS = ["x", "rt", "w", "r2a", "r2b", "vx", "vh", "fd", "fo", "fl", "td", "to", "tl", "wd", "wo", "ti", "wi",
         "y", "oc", "o0", "o1", "o2", "o3", "who"]
SEMAPHORES = ["qv", "qa", "qt", "qg", "af", "a1", "at", "a2", "aw", "loc"] + ["d_" + k for k in _DMAS]


def plan(T, topo, s):
    c = T.cores[s]
    near = [r for r in range(N) if r != s and topo.chip(T.cores[r]) == topo.chip(c)]

    def hops(r):
        a, b = topo.chip(c), topo.chip(T.cores[r])
        return 0 if topo.mates(a, b) else 1 if topo.same_plane(a, b) else 2
    far = sorted([r for r in range(N) if r != s and r not in near], key=lambda r: (hops(r), (r - s) % N))
    e = topo.engines(c, T.cores[far[0]])
    k = [x for x in topo.engines(c, T.cores[near[0]]) if x not in e][:2]
    one = {far[0]: e[0:1], far[1]: e[1:2], far[2]: e[2:3], far[3]: e[3:4], far[4]: e[4:6], far[5]: e[6:8], near[0]: k}
    two = {far[4]: e[4:5], far[5]: e[5:6], far[0]: e[6:7], far[1]: e[7:8], far[2]: e[0:2], far[3]: e[2:4], near[0]: k}
    return one, two, {**one, near[0]: e}


def rank_program(g, core, T, topo):
    me = T.rank_of(core)
    if me is None:
        return
    S = T.sem
    plans = [plan(T, topo, s) for s in range(N)]
    others = [r for r in range(N) if r != me]
    far = [r for r in others if topo.chip(T.cores[r]) != topo.chip(core)]
    near = [r for r in others if r not in far]
    eng = {"v": g.vector, "a": g.scalar, "t": g.tensor, "s": g.sync, "g": g}
    vec = g.vector
    V = {"set": vec.memset, "copy": vec.tensor_copy, "ts": vec.tensor_scalar, "tt": vec.tensor_tensor,
         "scan": vec.tensor_tensor_scan, "red": vec.tensor_reduce, "tr": vec.transpose, "qz": vec.quantize_mx}
    G = {"iota": g.iota, "sel": g.affine_select}
    cnt = {}
    seen = {q: {} for q in eng}
    wr, rd = {}, {}

    def need(q, evs):
        m = {}
        for sem, n in evs:
            m[sem] = max(n, m.get(sem, 0))
        for sem in sorted(m):
            if seen[q].get(sem, 0) < m[sem]:
                eng[q].wait_ge(S[sem], m[sem])
                seen[q][sem] = m[sem]

    def before(q, reads, writes, part):
        evs = [e for t in reads for e in wr[t]]
        if not part:
            evs += [e for t in writes for e in wr.get(t, []) + rd.get(t, [])]
        need(q, evs)

    def after(ev, reads, writes, part):
        for t in reads:
            rd.setdefault(t, []).append(ev)
        for t in writes:
            wr[t] = (wr.get(t, []) if part else []) + [ev]
            if not part:
                rd[t] = []

    def op(q, f, args, reads=(), writes=(), part=False, **kw):
        before(q, reads, writes, part)
        sem = "q" + q
        cnt[sem] = cnt.get(sem, 0) + 1
        f(*args, **kw).then_inc(S[sem], 1)
        after((sem, cnt[sem]), reads, writes, part)

    def v(name, *args, **kw):
        op("v", V[name], args, **kw)

    def act(*args, **kw):
        op("a", g.scalar.activation, args, **kw)

    def mm(*args, **kw):
        op("t", g.tensor.matmul_mx, args, **kw)

    def gp(name, *args, **kw):
        op("g", G[name], args, **kw)

    def dma(q, key, out, in_, reads=(), writes=(), part=False):
        before(q, reads, writes, part)
        eng[q].dma_start(out, in_).then_inc(S["d_" + key], 16)
        cnt["d_" + key] = 16
        after(("d_" + key, 16), reads, writes, part)

    def send(to, which, sem, src, dst, reads):
        need("g", [e for t in reads for e in wr[t]])
        tr = []
        for d in to:
            es = plans[me][which][d]
            rid, pid, _ = topo.addr(T.cores[d])
            tr.append(RemoteDMATransfer(dst_ids=[DstId(rid=rid, pnc=pid)], dma_engine_mask=sum(1 << e for e in es),
                                        remote_sem=S[sem], src=src(d), dst=dst(d)))
            cnt["loc"] = cnt.get("loc", 0) + len(es)
        g.remote_dma_fused(tr, local_sem=S["loc"])

    def lands(tag, sem, *which):
        cnt[sem] = sum(len(plans[s][w][me]) for s in others for w in which)
        wr[tag].append((sem, cnt[sem]))

    u8, u32 = dt.uint8, dt.uint32
    blk = [slice(32 * b, 32 * b + 32) for b in range(N)]
    half = [slice(128 * h, 128 * h + 128) for h in range(4)]
    row = [slice(SL * h, SL * h + SL) for h in range(2)]

    dma("s", "x", T.xt[:, 0:512], T.x[:, :], writes=["xt"], part=True)
    dma("a", "rt", T.rtt[:, 0:4 * N], T.rt[:, 0:4 * N], writes=["rtt"], part=True)
    dma("s", "w", T.wt[:, :], T.w[:, :], writes=["wt"])
    if me > 0:
        dma("a", "r2a", T.r2t[:, 0:4 * me], T.r2[:, 0:4 * me], writes=["r2t"], part=True)
    dma("a", "r2b", T.r2t[:, 4 * me:4 * N], T.r2[:, 4 * me + 4:4 * N + 4], writes=["r2t"], part=True)

    fl = {"allow_small_or_imprecise_dtypes": True}
    gp("iota", T.pp[:, :], [[0, 8]], 0, 1, writes=["pp"])
    gp("iota", T.tokv[:, :], [[1, 144]], 0, 0, writes=["tokv"], **fl)
    gp("iota", T.m1[:, :], [[0, 128]], -1, 0, writes=["m1"], **fl)
    gp("iota", T.cc[:, :], [[1, 8]], 0, 0, writes=["cc"])
    gp("iota", T.io32[:, :], [[1, 32]], 0, 0, writes=["io32"], **fl)
    v("set", T.zb[:, :], 0.0, writes=["zb"])
    v("set", T.rtt[:, 4 * N:512], 0.0, writes=["rtt"], part=True)
    v("set", T.xt[:, 512:520], 0.0, writes=["xt"], part=True)
    v("set", T.neg8[:, :], -9e29, writes=["neg8"])
    v("ts", T.pb[:, :], T.pp[:, :], 4, 14, A.logical_shift_right, A.bitwise_and, reads=["pp"], writes=["pb"])
    v("ts", T.p15[:, :], T.pp[:, :], 15, None, A.bitwise_and, reads=["pp"], writes=["p15"])
    for u in range(2):
        v("ts", T.ecol[:, u:u + 1], T.pb[:, 0:1], float(u), None, A.add, reads=["pb"], writes=["ecol"], part=True)
        v("ts", T.thr1[:, u:u + 1], T.p15[:, 0:1], 16.0 * u, None, A.add, reads=["p15"], writes=["thr1"], part=True)
    for k in range(4):
        act(T.rsA[:, half[k]], T.zb[:, :], F.Identity, reads=["zb"], writes=["rsA1"], part=True, bias=1.0)
    act(T.rsA[:, 0:512:128], T.zb[:, 0:4], F.Copy, reads=["zb", "rsA1"], writes=["rsA"])
    act(T.thrh[:, :], T.thr1[:, :], F.Identity, reads=["thr1"], writes=["thrh"], bias=0.5)
    dma("a", "wo", T.whol[me:me + 1, 0:CB, 0], T.m1[0:1, 0:CB], reads=["m1"], writes=["whol"], part=True)
    dma("a", "wi", T.whod[:, :, 0], T.m1[0:N, :], reads=["m1"], writes=["whod"])
    dma("a", "ti", T.tokd[:, :, 0], T.zb[0:N, :], reads=["zb"], writes=["tokd"])

    v("qz", T.rq[:, :], T.rs[:, :], T.rtt[:, :], reads=["rtt"], writes=["rq"])
    v("qz", T.xq[:, 0:130], T.xs[:, 0:130], T.xt[:, :], reads=["xt"], writes=["xq"])
    mm(T.p0[:, 0:128], T.xq[:, 0:128], T.xs[:, 0:128], T.rq[:, :], T.rs[:, :], True, True, reads=["xq", "rq"], writes=["p0"])
    v("scan", T.R[:, :], T.p0[:, 0:8], T.neg8[:, :], -9e29, A.max, A.max, reads=["p0", "neg8"], writes=["R"])
    act(T.mj[:, 0:8], T.R[:, :], F.Sign, reads=["R"], writes=["first"], bias=T.R[:, 7:8], scale=-1.0, accum_out=T.first[:, 0:1])
    v("ts", T.fb[:, :], T.zb[:, 0:32], T.first[:, 0:1], None, A.add, reads=["zb", "first"], writes=["fb"])
    dma("s", "fd", T.fd[:, :], T.fb[:, 0:1], reads=["fb"], writes=["fd"])
    dma("s", "fo", T.fl[me], T.fb[:, 0:1], reads=["fb"], writes=["fl"], part=True)
    send(near, 2, "af", lambda d: T.fb[:, 0:1], lambda d: T.fl[me], ["fb"])
    for a in range(4):
        v("tr", T.fr[0:32, blk[a]], T.fb[blk[a], :], reads=["fb"], writes=["fr"], part=True)
    act(T.fr[blk[3], :], T.fr[0:32, :], F.Copy, reads=["fr"], writes=["frc"])
    for b in range(1, 3):
        v("copy", T.fr[blk[b], :], T.fr[0:32, :], reads=["fr"], writes=["fra"], part=b > 1)
    for u in range(2):
        v("ts", T.M1[:, half[u]], T.fr[:, :], T.ecol[:, u:u + 1], None, A.is_equal,
          reads=["fr", "fra", "frc", "ecol"], writes=["M1%d" % u])
    for u in range(2):
        v("scan", T.C1[:, half[u]], T.rsA[:, half[u]], T.M1[:, half[u]], 0.0, A.mult, A.add, reads=["rsA", "M1%d" % u], writes=["C1%d" % u])
    for h in range(2):
        act(T.L1[:, half[2 + h]], T.C1[:, half[0]], F.Sign, reads=["C10", "thrh"], writes=["sa"], part=True,
            bias=T.thrh[:, h:h + 1], scale=-1.0, accum_out=T.sa[:, h:h + 1])
        v("ts", T.L1[:, half[h]], T.C1[:, half[1]], T.thr1[:, h:h + 1], None, A.is_le, reads=["C11", "thr1"], writes=["L1%d" % h])
    for h in range(2):
        v("scan", T.S1[:, half[h]], T.rsA[:, half[h]], T.L1[:, half[h]], 0.0, A.mult, A.add, reads=["rsA", "L1%d" % h], writes=["S1"], part=True)
    for b in range(4):
        act(T.lf1[0:32, 4 * b:4 * b + 2], T.sa[blk[b], 0:2], F.Identity, reads=["sa"], writes=["lf1"], part=True, bias=64.0, scale=0.5)
        v("copy", T.lf1[0:32, 4 * b + 2:4 * b + 4], T.S1[blk[b], 127:256:128], reads=["S1"], writes=["lf1"], part=True)
    for b in range(4):
        v("copy", T.off1[blk[b], :], T.lf1[0:32, :], reads=["lf1"], writes=["off1"], part=True)
    O1 = ["off1", "xq"]
    ms = slice(2 * me, 2 * me + 2)
    v("copy", T.sq[:, :].bitcast(u32), T.xq[:, 0:130].bitcast(u32).indirect(T.off1[:, :]), reads=O1, writes=["sq"])
    act(T.ss[:, :], T.xs[:, 0:130].indirect(T.off1[:, :]), F.Copy, reads=O1, writes=["ss"])
    v("copy", T.xh[:, blk[me]].bitcast(u32), T.xq[:, 0:130].bitcast(u32).indirect(T.off1[:, ms]), reads=O1, writes=["xh"], part=True)
    act(T.xhs[:, blk[me]], T.xs[:, 0:130].indirect(T.off1[:, ms]), F.Copy, reads=O1, writes=["xh"], part=True)
    act(T.trow[:, :], T.tokv[:, :].indirect(T.off1[:, :]), F.Copy, reads=O1 + ["tokv"], writes=["trow"])

    send(far, 2, "af", lambda d: T.fd[:, :], lambda d: T.fl[me], ["fd"])
    send(others, 0, "a1", lambda d: T.sq[:, blk[d]].bitcast(u8), lambda d: T.xh[:, blk[me]].bitcast(u8), ["sq"])
    send(others, 1, "a1", lambda d: T.ss[:, blk[d]], lambda d: T.xhs[:, blk[me]], ["ss"])
    lands("fl", "af", 2)
    dma("s", "fl", T.frl[0:8, :], T.fl[:, :, 0], reads=["fl"], writes=["frl"])
    dma("s", "td", T.tokd[:, 0:CAPP, 0], T.trow[0:1, :], reads=["trow"], writes=["tokd"])
    dma("s", "to", T.tokl[me:me + 1, 0:CAPP, 0], T.trow[0:1, blk[me]], reads=["trow"], writes=["tokl"], part=True)

    act(T.sgn[:, :], T.wt[:, 0:2 * SL], F.Identity, reads=["wt"], writes=["sgn1"], bias=1.0, scale=0.0)
    for t in range(4):
        act(T.r8t[:, t:512:4], T.zb[:, :], F.Identity, reads=["r2t", "zb"], writes=["r8t"], part=True, bias=T.r2t[:, 28 + t:29 + t])
    act(T.one[:, :], T.wt[:, 0:2 * SL], F.Identity, reads=["wt"], writes=["one1"], bias=1.0, scale=0.0)
    act(T.tokw[:, :], T.wt[:, 0:648], F.Identity, reads=["wt"], writes=["tokm"], bias=-1.0, scale=0.0)
    v("qz", T.wq[:, :], T.ws[:, :], T.wt[:, :], reads=["wt"], writes=["wq"])
    v("set", T.zt[:, :], 0.0, writes=["zt"])
    v("set", T.r2t[:, 4 * N:512], 0.0, writes=["r2z"])
    v("set", T.ht[:, 1024:1032], 0.0, writes=["htz"])
    v("copy", T.offz[:, :], T.thr1[:, :], reads=["thr1"], writes=["offz"])
    v("qz", T.xh[:, 256:384], T.xhs[:, 256:384], T.zt[:, :], reads=["zt"], writes=["xhz"])
    v("qz", T.r2q[:, :], T.r2s[:, :], T.r2t[:, :], reads=["r2t", "r2z"], writes=["r2q"])
    v("ts", T.p31[:, :], T.pp[:, :], 31, None, A.bitwise_and, reads=["pp"], writes=["p31"])
    v("set", T.nb[:, :], 0.0, writes=["nb"])
    v("qz", T.r8q[:, :], T.r8s[:, :], T.r8t[:, :], reads=["r8t"], writes=["r8q"])
    v("copy", T.ccol[:, :], T.p31[:, 0:1], reads=["p31"], writes=["ccol"])
    OZ = ["offz", "xhz"]
    v("copy", T.l2q[:, blk[me]].bitcast(u32), T.xh[:, 256:384].bitcast(u32).indirect(T.offz[:, :]), reads=OZ, writes=["l2"], part=True)
    v("copy", T.l2s[:, blk[me]], T.xhs[:, 256:384].indirect(T.offz[:, :]), reads=OZ, writes=["l2"], part=True)
    v("ts", T.ig[:, :], T.cc[:, :], 32.0, float(CB), A.mult, A.add, reads=["cc"], writes=["ig"])
    v("ts", T.mgt[:, :], T.ecol[:, :], float(me), -1.0, A.is_gt, A.mult, reads=["ecol"], writes=["mgt"])
    v("tt", T.ih[:, :], T.ig[:, :], T.p15[:, :], A.add, reads=["ig", "p15"], writes=["ih"])
    v("tt", T.mct[:, :], T.ecol[:, :], T.mgt[:, :], A.add, reads=["ecol", "mgt"], writes=["mct"])
    v("copy", T.offh[:, :], T.ih[:, :], reads=["ih"], writes=["offh"])
    v("ts", T.mcol[:, :], T.mct[:, :], 1.0, None, A.add, reads=["mct"], writes=["mcol"])
    v("set", T.lim8[:, 0:7], 9e29, writes=["lim8"], part=True)
    v("set", T.lim8[:, 7:8], -9e29, writes=["lim8"], part=True)
    v("set", T.c128[:, :], 128.0, writes=["c128"])
    v("set", T.one[:, 0:2 * SL:SL], 0.0, reads=["one1"], writes=["one"])
    for h in range(2):
        k = slice(SL * h + 128 * h, SL * h + 128 * h + 128)
        gp("sel", T.sgn[:, k], T.sgn[:, k], [[-1, 128]], A.not_equal, -1.0, 0, 1, reads=["sgn1"], writes=["sgn"], part=True)
    send(others, 0, "at", lambda d: T.tokd[d], lambda d: T.tokl[me], ["tokd"])

    v("ts", T.feq[0:8, :], T.frl[0:8, :], float(me), None, A.is_equal, reads=["frl"], writes=["feq"])
    red(v, T.nb[0:8, :], T.feq[0:8, :], reads=["feq"], writes=["nb"])
    v("ts", T.nbb[:, :], T.zb[0:32, 0:32], T.nb[:, 0:1], None, A.add, reads=["zb", "nb"], writes=["nbb"])
    v("tr", T.nrep[0:32, :], T.nbb[:, :], reads=["nbb"], writes=["nrep"])
    for b in range(1, 4):
        v("copy", T.nrep[blk[b], :], T.nrep[0:32, :], reads=["nrep"], writes=["nrepa"], part=True)
    NR = ["nrep", "nrepa"]

    def pens(*ranks):
        for s in ranks:
            v("ts", T.pen[:, blk[s]], T.io32[:, :], T.nrep[:, s:s + 1], BIG, A.is_ge, A.mult,
              reads=NR + ["io32"], writes=["pen%d" % (s // 4)], part=True)

    def nbs():
        act(T.nrepb[:, :], T.nrep[:, 0:8], F.Identity, reads=NR, writes=["nrepb"], bias=BIG, scale=-BIG)

    def pns(*ranks):
        for s in ranks:
            act(T.pen[:, blk[s]], T.io32[:, :], F.Relu, reads=["nrepb", "io32"], writes=["pen%d" % (s // 4)], part=True,
                bias=T.nrepb[:, s:s + 1], scale=BIG)

    def pcs(*blocks):
        for a in blocks:
            v("ts", T.Rm[blk[a], 0:18:9], T.nrep[blk[a], a:8:4], T.ccol[blk[a], 0:1], -9e29, A.is_gt, A.mult,
              reads=NR + ["ccol"], writes=["Rmc"], part=True)
    fill = {(0, 0): [(nbs,), (pns, 4)], (0, 2): [(pns, 5)], (1, 0): [(pns, 6, 7)],
            (0, 1): [(pens, 0, 1)], (0, 3): [(pens, 2)], (1, 1): [(pens, 3), (pcs, 0)], (1, 3): [(pcs, 1)], (1, 4): [(pcs, 2, 3)]}
    lands("tokl", "at", 0)
    dma("s", "tl", T.tokr[0:1, :], T.tokl[:, 0:CAPP, 0], reads=["tokl"], writes=["tokr"])
    dma("s", "vx", T.vxt[:, :], T.vx[:, :], writes=["vxt"])
    dma("s", "vh", T.vht[:, :], T.vh[:, :], writes=["vht"])

    lands("xh", "a1", 0, 1)
    P = [[T.p1, T.p2, T.p3, T.p4], [T.p0, T.p5, T.p6, T.p7]]
    B = [["p1", "p2", "p3", "p4"], ["p0", "p5", "p6", "p7"]]
    for h in range(2):
        for i in range(4):
            mm(P[h][i][:, 0:128], T.wq[:, half[i]], T.ws[:, half[i]], T.xh[:, half[h]], T.xhs[:, half[h]], True, True,
               reads=["wq", "xh"], writes=[B[h][i]])
    ROW, rw, PE, pe = [T.p1, T.p4], ["p1", "p4"], [T.p2, T.p3], ["p2", "p3"]

    def products(h):
        k = slice(HO + 128 * h, HO + 128 * h + 128)
        mm(ROW[h][:, 0:128], T.r8q[:, :], T.r8s[:, :], T.xh[:, k], T.xhs[:, k], True, True, reads=["r8q", "h%d" % h], writes=[rw[h]])
        mm(PE[h][:, 0:128], T.xh[:, k], T.xhs[:, k], T.r2q[:, :], T.r2s[:, :], True, True, reads=["r2q", "h%d" % h], writes=[pe[h]])
    for h in range(2):
        e = 512 * (h + 1)
        for i in range(4):
            o = T.ht[:, 512 * h + i:e:4]
            if i % 2:
                v("ts", o, P[h][i][:, 0:128], 0.0, 0.0625, A.max, A.mult, reads=[B[h][i]], writes=["ht%d" % h], part=True)
            else:
                act(o, P[h][i][:, 0:128], F.Relu, reads=[B[h][i]], writes=["ht%d" % h], part=True, scale=0.0625)
            for f, *n in fill.get((h, i), []):
                f(*n)
        k = slice(HO + 128 * h, XW if h else HO + 128)
        v("qz", T.xh[:, k], T.xhs[:, k], T.ht[:, 512 * h:e + 8 * h], reads=["ht%d" % h, "htz"], writes=["h%d" % h])
        products(h)
        for f, *n in fill.get((h, 4), []):
            f(*n)

    def second(h):
        k = 9 * h
        v("scan", T.Rm[:, k + 1:k + 9], T.lim8[:, :], PE[h][:, 0:8], -9e29, A.min, A.max, reads=[pe[h], "lim8"], writes=["Rm%d" % h])

    def away(h):
        v("tt", T.E1[:, half[h]], ROW[h][:, 0:128], T.pen[:, half[h]], A.add, reads=[rw[h], "pen%d" % h], writes=["E1"], part=True)
    second(0)
    away(0)
    away(1)
    second(1)

    def number(h):
        k = 9 * h
        act(T.mj[:, 8 * h:8 * h + 8], T.Rm[:, k:k + 8], F.Sign, reads=["Rm%d" % h, "Rmc"], writes=["mm%d" % h],
            bias=T.Rm[:, k + 7:k + 8], scale=-1.0, accum_out=T.mm[:, h:h + 1])
        act(T.mp[:, h:h + 1], T.mm[:, h:h + 1], F.Copy, reads=["mm%d" % h], writes=["mp%d" % h])
    number(0)
    for h in range(2):
        e8 = T.Rm[:, 9 * h + 8:9 * h + 9]
        act(T.SJ[:, row[h]], T.E1[:, :], F.Sign, reads=["E1", "Rm%d" % h], writes=["sg%d" % h],
            bias=e8, scale=-1.0, accum_out=T.sg[:, h:h + 1])
        v("ts", T.EQ[:, row[h]], T.E1[:, :], e8, None, A.is_equal, reads=["E1", "Rm%d" % h], writes=["EQ%d" % h])
    number(1)

    def rank(h):
        v("scan", T.FS[:, row[h]], T.sgn[:, row[h]], T.EQ[:, row[h]], T.sg[:, h:h + 1], A.mult, A.add,
          reads=["sgn", "EQ%d" % h, "sg%d" % h], writes=["FS%d" % h])
    rank(0)
    rank(1)
    for h in range(2):
        v("ts", T.fb2[:, blk[h]], T.c128[:, :], T.FS[:, SL * h + SL - 1:SL * h + SL], T.mp[:, h:h + 1], A.is_lt, A.mult,
          reads=["c128", "FS%d" % h, "mp%d" % h], writes=["fb2"], part=True)
    for a in range(4):
        v("tr", T.fr2[0:32, a, :], T.fb2[blk[a], :], reads=["fb2"], writes=["fr2"], part=True)
    act(T.fr2[blk[3], :, :], T.fr2[0:32, :, :], F.Copy, reads=["fr2"], writes=["fr2c"])
    for b in range(1, 3):
        v("copy", T.fr2[blk[b], :, :], T.fr2[0:32, :, :], reads=["fr2"], writes=["fr2a"], part=b > 1)
    for u in range(2):
        for h in range(2):
            v("ts", T.M2[:, half[2 * u + h]], T.fr2[:, :, blk[h]], T.mcol[:, u:u + 1], None, A.is_equal,
              reads=["fr2", "fr2a", "fr2c", "mcol"], writes=["M2%d" % u], part=True)
    for u in range(2):
        v("scan", T.C2[:, row[u]], T.one[:, row[u]], T.M2[:, row[u]], 0.0, A.mult, A.add, reads=["one", "M2%d" % u], writes=["C2%d" % u])
    act(T.SJ[:, row[0]], T.C2[:, row[0]], F.Sign, reads=["C20", "thrh"], writes=["sa2"],
        bias=T.thrh[:, 0:1], scale=-1.0, accum_out=T.sa[:, 2:3])
    for h in range(2):
        v("ts", T.L2[:, half[h]], T.C2[:, half[2 + h]], T.thr1[:, 0:1], None, A.is_le, reads=["C21", "thr1"], writes=["L2%d" % h])
    for h in range(2):
        v("scan", T.S2[:, half[h]], T.one[:, half[h]], T.L2[:, half[h]], 0.0, A.mult, A.add, reads=["one", "L2%d" % h], writes=["S2"], part=True)
    for b in range(4):
        act(T.lf2[0:32, 2 * b:2 * b + 1], T.sa[blk[b], 2:3], F.Identity, reads=["sa2"], writes=["lf2"], part=True, bias=128.0, scale=0.5)
        v("tt", T.lf2[0:32, 2 * b + 1:2 * b + 2], T.S2[blk[b], 127:128], T.S2[blk[b], 255:256], A.add, reads=["S2"], writes=["lf2"], part=True)
    for s in range(N):
        act(T.tokw[0:1, blk[s]], T.tokr[0:1, blk[s]], F.Identity, reads=["tokr", "tokm"], writes=["tokw"], part=True, bias=float(TK * s))
    for b in range(4):
        v("copy", T.off2[blk[b], 0:16:2], T.lf2[0:32, :], reads=["lf2"], writes=["off2%d" % (b // 2)], part=True)
    for k in range(2):
        q = slice(64 * k, 64 * k + 64)
        v("ts", T.off2[q, 1:16:2], T.off2[q, 0:16:2], float(HO), None, A.add, reads=["off2%d" % k], writes=["off2a"], part=True)
    O2 = ["off20", "off21", "off2a"]
    XR = O2 + ["xh", "xhz", "h0", "h1"]
    v("copy", T.s2q[:, :].bitcast(u32), T.xh[:, 0:XW].bitcast(u32).indirect(T.off2[:, :]), reads=XR, writes=["s2q"])
    act(T.wr[:, :], T.tokw[:, 0:XW].indirect(T.off2[:, :]), F.Copy, reads=O2 + ["tokw", "tokm"], writes=["wr"])
    act(T.s2s[:, :], T.xhs[:, 0:XW].indirect(T.off2[:, :]), F.Copy, reads=XR, writes=["s2s"])
    send(others, 0, "a2", lambda d: T.s2q[:, blk[d]].bitcast(u8), lambda d: T.l2q[:, blk[me]].bitcast(u8), ["s2q"])
    send(others, 1, "a2", lambda d: T.s2s[:, blk[d]], lambda d: T.l2s[:, blk[me]], ["s2s"])

    dma("s", "wd", T.whod[:, 0:2 * CB, 0], T.wr[0:1, :], reads=["wr"], writes=["whod"])
    send(others, 0, "aw", lambda d: T.whod[d], lambda d: T.whol[me], ["whod"])
    v("qz", T.vxq[:, :], T.vxs[:, :], T.vxt[:, :], reads=["vxt"], writes=["vxq"])
    v("qz", T.vhq[:, :], T.vhs[:, :], T.vht[:, :], reads=["vht"], writes=["vhq"])

    lands("l2", "a2", 0, 1)
    Y, yt = [T.p0, T.p5], ["p0", "p5"]
    for q in range(2):
        n, t = (144, 128)[q], yt[q]
        k, j = slice(112 * q, 112 * q + n), slice(112 * q + CB, 112 * q + CB + n)
        mm(Y[q][:, 0:n], T.vxq[:, :], T.vxs[:, :], T.l2q[:, k], T.l2s[:, k], True, False, reads=["vxq", "l2"], writes=[t])
        mm(Y[q][:, 0:n], T.vhq[:, :], T.vhs[:, :], T.l2q[:, j], T.l2s[:, j], False, True, reads=["vhq", "l2"], writes=[t], part=True)
    v("copy", T.hq[:, :].bitcast(u32), T.l2q[:, :].bitcast(u32).indirect(T.offh[:, :]), reads=["l2", "offh"], writes=["hq"])
    act(T.hs[:, :], T.l2s[:, :].indirect(T.offh[:, :]), F.Copy, reads=["l2", "offh"], writes=["hs"])
    for a in range(N):
        k = 32 * a - 112 * (a // 5)
        o, i = T.ysb[:, CB * a:CB * a + CB], Y[a // 5][:, k:k + CB]
        if a < 5:
            v("copy", o, i, reads=[yt[0]], writes=["ysb"], part=True)
        else:
            act(o, i, F.Copy, reads=[yt[1]], writes=["ysb"], part=True)
    dma("s", "oc", T.oc[:, :], T.hq[:, :].bitcast(u8), reads=["hq"], writes=["oc"])
    for k in range(4):
        dma("s" if k < 2 else "a", "o%d" % k, T.osc[4 * k:4 * k + 4, :], T.hs[32 * k:32 * k + 4, :], reads=["hs"], writes=["osc%d" % k])
    dma("s", "y", T.y[:, :], T.ysb[:, :], reads=["ysb"], writes=["y"])
    lands("whol", "aw", 0)
    dma("s", "who", T.who[0:1, :], T.whol[:, 0:CB, 0], reads=["whol"], writes=["who"])
    for sem in sorted(cnt):
        if max(seen[q].get(sem, 0) for q in eng) < cnt[sem]:
            need("a" if sem in ("d_o2", "d_o3") else "s" if sem[:2] == "d_" else "g", [(sem, cnt[sem])])


def red(v, out, in_, **kw):
    v("red", out, in_, axis=AxisListType.X, op=A.add, **kw)
